import numpy as np, ml_dtypes
CORES = [16,17,18,19,32,33,34,35]
N = 8
import mx_ref
BF = ml_dtypes.bfloat16
def gentries(a):
    return np.ascontiguousarray(a.reshape(8, 16, -1).transpose(0, 2, 1)).reshape(8, -1)
def gtable(e):
    e = np.asarray(e); return np.ascontiguousarray(e.reshape(8, -1, 16).transpose(0, 2, 1)).reshape(128, -1).astype(np.int32)
def gcols(t, e):
    v = np.concatenate([t.reshape(8, 16, -1, 4), np.zeros((8, 16, 1, 4), BF)], axis=2)
    return np.ascontiguousarray(np.stack([v[g][:, e[g]] for g in range(8)])).reshape(128, -1)
def tile(rs):
    return np.stack(rs, axis=2).reshape(128, -1).astype(BF)
def pick(q, e):
    c = np.concatenate([q[0].reshape(128, -1, 4), np.zeros((128, 1, 4), np.uint8)], axis=1); s = np.concatenate([q[1], np.ones((16, 1), np.uint8)], axis=1)
    return (np.ascontiguousarray(c[:, e].reshape(128, -1)), np.ascontiguousarray(s[:, e]))
def join(*qs):
    return (np.concatenate([q[0] for q in qs], axis=1), np.concatenate([q[1] for q in qs], axis=1))
def put(q, e, v):
    c, s = q[0].reshape(128, -1, 4).copy(), q[1].copy(); c[:, e] = v[0].reshape(128, -1, 4); s[:, e] = v[1]
    return (c.reshape(128, -1), s)
def pk(c, s):
    return (np.ascontiguousarray(c), mx_ref.live(s))
def emit(q):
    return q[0], q[1]
def packed(v, rng):
    q = [mx_ref.quantize(np.ascontiguousarray(v[r])) for r in range(N)]
    return np.stack([a for a, b in q]), np.stack([mx_ref.plane(b, rng) for a, b in q])
def values_of_codes():
    e, c = np.zeros((128, 128, 4), np.float32), np.zeros((128, 2, 4), np.uint8)
    e[np.arange(128), np.arange(128), 0] = 1
    c[:127, :, 0] = np.arange(256).reshape(2, 128).T[:127]
    return mx_ref.matmul(mx_ref.quantize(e.reshape(128, 512).astype(BF)), (c.reshape(128, 8), np.full((16, 2), 127, np.uint8))).T.reshape(-1).astype(np.float64)
CODE_VALUE, SCALE_VALUE = values_of_codes(), 2.0 ** (np.arange(256) - 127.0)
def decode(q):
    return (CODE_VALUE[q[0]].reshape(16, 8, -1, 4) * SCALE_VALUE[q[1]][:, None, :, None] + 0.0).reshape(128, -1).astype(np.float32)
def f(rng, *shape):
    return mx_ref.flush((rng.standard_normal(shape, dtype=np.float32) * np.exp2(rng.integers(-2, 3, shape[:-1] + (1,)))).astype(BF))
def wide(rng, *shape, cols=0):
    v = rng.standard_normal(shape, dtype=np.float32) * np.exp2(rng.integers(-12, 13, shape)).astype(np.float32)
    if cols: v *= np.repeat(np.exp2(rng.integers(-cols, cols + 1, shape[:-2] + (1, shape[-1] // 4))) * (rng.random(shape[:-2] + (1, shape[-1] // 4)) > 0.0625), 4, axis=-1).astype(np.float32)
    return mx_ref.flush(v.astype(BF))
C, M, WIDTH = 256, 16, 16
ROUNDS = 3
def big(v):
    v = v.astype(np.float32)
    v[np.abs(v) < np.float32(2.0 ** -16)] = 0
    return v.astype(BF)
def numbers_of(rng):
    return {"x": np.array(f(rng, N, 128, 4 * C)), "u": np.array(f(rng, N, 128, 512)), "v": np.array(f(rng, N, 128, 512))}
def towers(rng):
    return np.stack([gtable(np.stack([rng.permutation(C) for g in range(8)])) for r in range(N)])
def layers(rng):
    w = f(rng, N, 128, 2048).astype(np.float32).reshape(N, 128, 512, 4)
    w[rng.random(w.shape) < 0.9375] = 0
    m = np.searchsorted(28.0 * 2.0 ** np.arange(-20.0, 30.0), np.sum(np.abs(w), axis=(1, 3), keepdims=True))
    return np.array(mx_ref.flush((w * (2.0 ** (20.0 - m)).astype(np.float32)).astype(BF))).astype(np.float32)
def mirror(k):
    w, i = np.zeros((N, 128, 4, 128, 4), np.float32), np.arange(128)
    for b in range(4): w[:, i, b, i, b] = 32 * k[:, None]
    return w.reshape(N, 128, 512, 4)
def weights(rng, w):
    c, s = packed(np.ascontiguousarray(w).reshape(N, 128, 2048).astype(BF), rng)
    return {"wc": c, "ws": s}
def setup_inputs(rng):
    return {**numbers_of(rng), "tw": towers(rng), **weights(rng, layers(rng))}
def setup_inputs_ties(rng):
    d = numbers_of(rng)
    x = d["x"].astype(np.float32).reshape(N, 8, 16, C, 4)
    x[:, :, :8] = 0
    x[:, :, 0, :, 0] = rng.integers(0, 4, (N, 8, C))
    n = (N, 8, 8, C, 4)
    a = (1 + (2 * rng.integers(0, 64, n) + 1) / 128) * np.exp2(rng.integers(-14, -7, n)) * rng.choice([-1.0, 1.0], n)
    a[:, :, 0, :, 0] = 1.96875
    x[:, :, 8:] = a * np.exp2(rng.integers(-2, 3, (N, 8, 1, 1, 1)))
    u = d["u"].reshape(N, 128, 128, 4)
    u[:, :, ::16] = 0
    o = rng.permutation(N)
    for r in range(N):
        for h in range(0, 128, 16): u[r, h, h, 0] = 0.0 if r == o[0] else -1.0 if r in (o[1], o[3]) else 1.0
    w = layers(rng)
    w.reshape(N, 128, 4, 8, 16, 4)[:, :, :, :, :8] = 0
    return {"x": x.reshape(N, 128, 4 * C).astype(BF), "u": u.reshape(N, 128, 512), "v": d["v"], "tw": towers(rng), **weights(rng, w)}
def setup_inputs_near(rng):
    d = numbers_of(rng)
    x = d["x"].astype(np.float32).reshape(N, 8, 16, C, 4)
    u = d["u"].reshape(N, 128, 128, 4)
    u[:, :, ::16] = 0
    x[:, :, 0] = 0
    x[:, :, 8:] = 0
    s = rng.integers(0, 16, (N, 8, C))
    o = rng.permutation(8) % 4
    turn = np.arange(N) % 2 == rng.integers(2)
    w = mirror(np.ones(N)).reshape(N, 128, 4, 128, 4)
    for g in range(8):
        h = 16 * g
        if o[g] < 3:
            k = 2.0 ** -30 if o[g] == 2 else 1.0
            x[:, g, 0, :, 0] = -1.0 if o[g] == 1 else 1.0
            x[:, g, 8] = ((s[:, g, :, None] >> np.arange(4)) & 1) * np.exp2(np.arange(4) - 23.0)
            x[:, g, 11, :, 0] = 2.0 ** -10
            u[:, h, h, 0] = k
            u[:, h + 8, h] = k
            u[:, h + 11, h, 0] = k
            if o[g] == 0:
                x[turn, g, 8] = 0
                u[turn, h + 8, h] = -4.0
        else:
            x[:, g, 9:11, :, 0] = (1 + rng.integers(0, 8, (N, 2, C)) / 8) * 2.0 ** -30
            x[:, g, 12, :, 0] = 2.0 ** -30
            u[:, h + 9, h, 0] = -2.0 ** -30
            u[:, h + 10, h, 0] = 1.125 * 2.0 ** -30
            x[turn, g, 9:11] = 0
            u[turn, h + 9, h, 0] = 2.0 ** -30
            u[turn, h + 10, h, 0] = -1.125 * 2.0 ** -30
            for i in (h + 9, h + 10): w[turn, i, :, i] *= np.float32(2.0 ** -9)
    far = rng.permutation(np.nonzero(o < 3)[0])[:4]
    for r in range(N):
        for g in far: x[r, g, 0, rng.integers(C), 0] = 2.0 ** 30 * rng.choice([-1.0, 1.0])
    return {"x": x.reshape(N, 128, 4 * C).astype(BF), "u": u.reshape(N, 128, 512), "v": d["v"], "tw": towers(rng), **weights(rng, w)}
def setup_inputs_huge(rng):
    d = numbers_of(rng)
    o = rng.permutation(N)
    c = rng.choice([-1.0, 1.0], N)
    x = (0.6 + 0.4 * rng.random((N, 128, C, 4))) * 2.0 ** 30 * c[:, None, None, None]
    x[o < N // 2] *= rng.choice([-1.0, 1.0], (N // 2, 1, C, 1))
    u = d["u"].astype(np.float32).reshape(N, 128, 128, 4)
    k = np.stack([rng.permutation(8) % 2 * 2.0 - 1.0 for r in range(N)])
    u[:, :, ::16] = 2.0 ** 30 * (1 - 0.1 * rng.random((N, 128, 8, 4))) * k[:, None, :, None]
    e = int(np.argmax(o))
    a = np.where(rng.random((128, C, 4)) < rng.random((1, C, 1)), 0.9375, 1.0)
    a[::8, :, 0] = 1.0
    x[e] = a * 2.0 ** 30 * c[e]
    u[e, :, ::16] = 2.0 ** 30 * k[e][None, :, None]
    return {"x": x.astype(np.float32).reshape(N, 128, 4 * C).astype(BF), "u": u.reshape(N, 128, 512).astype(BF), "v": d["v"], "tw": towers(rng), **weights(rng, mirror(c * np.roll(c, 1)))}
def setup_inputs_ends(rng):
    d = numbers_of(rng)
    s, k0 = rng.choice([-1.0, 1.0]), int(rng.integers(4))
    x = d["x"].astype(np.float32).reshape(N, 128, C, 4)
    u = d["u"].astype(np.float32).reshape(N, 128, 128, 4)
    w, m, p = layers(rng), mirror(np.ones(N)), []
    for r in range(N):
        k = (r + k0) % 4
        c = (rng.permutation(8) % 2 * 2.0 - 1.0)[None, :, None]
        e = np.stack([rng.permutation(C)] * 8)
        if k == 0:
            x[r], w[r], u[r, :, ::16] = s * 2.0 ** 30, 0.0, 2.0 ** 30 * c
            e[:] = np.arange(C)
        elif k == 1:
            x[r], w[r], u[r, :, ::16] = s * 2.0 ** -30, m[r], 2.0 ** -30 * c
            e[:] = np.arange(C)[::-1]
        elif k == 2:
            x[r] = 2.0 ** 30 * rng.choice([-1.0, 1.0], (1, C, 1))
            w[r] = 0.0625 * rng.choice([-1.0, 1.0], (1, 512, 1))
            u[r, :, ::16] = 2.0 ** 30 * c
        else:
            for g in range(8): e[g] = np.roll(np.arange(C), g)
        p.append(gtable(e))
    d["v"] = (np.where(d["v"] < 0, -1.0, 1.0) * np.where(rng.permutation(N) % 2, 2.0 ** -30, 2.0 ** 30)[:, None, None]).astype(np.float32).astype(BF)
    return {"x": x.reshape(N, 128, 4 * C).astype(BF), "u": u.reshape(N, 128, 512).astype(BF), "v": d["v"], "tw": np.stack(p), **weights(rng, w)}
def setup_inputs_spread(rng):
    d = setup_inputs(rng)
    d["x"] = big(wide(rng, N, 128, 4 * C, cols=4))
    return d
def check_inputs(d):
    b = []
    for k in ("x", "u", "v"):
        a = np.abs(d[k].astype(np.float32))
        if not (np.isfinite(a).all() and ((a == 0) | (a >= 2.0 ** -30) & (a <= 2.0 ** 30)).all()): b.append("a value of " + k)
    none, least, most = [emit(mx_ref.quantize(np.full((128, 16), k, np.float32).astype(BF)))[1][0, 0] for k in (0.0, 2.0 ** -30, 2.0 ** 30)]
    for r in range(N):
        if (np.sort(gentries(d["tw"][r]), axis=1) != np.arange(C)).any(): b.append("tw: a group's entries aren't a permutation")
        if ((d["wc"][r] == 0x7F) | (d["wc"][r] == 0xFF)).any(): b.append("wc: a code that is no number")
        s = mx_ref.live(d["ws"][r])
        if ((s != none) & ((s < least) | (s > most))).any(): b.append("ws: a scale out of range")
        elif not (np.sum(np.abs(decode(pk(d["wc"][r], d["ws"][r])).astype(np.float64)).reshape(128, 512, 4), axis=(0, 2)) <= 32).all(): b.append("W: the sizes of a column are beyond 32 together")
    return b
def reference(x, u, v, tw, wc, ws):
    qu = [mx_ref.quantize(u[r]) for r in range(N)]
    lay = [pk(wc[r], ws[r]) for r in range(N)]
    now = [x[r] for r in range(N)]
    base = [gentries(tw[r]).reshape(8, M, WIDTH) for r in range(N)]
    top = [gentries(tw[r]).reshape(8, M, WIDTH) for r in range(N)]
    up = np.zeros((N, 8, C), np.int64)
    for t in range(ROUNDS):
        h = WIDTH >> (t + 1)
        own, ends = [], []
        for r in range(N):
            q = mx_ref.quantize(now[r])
            s = mx_ref.matmul(qu[r], q)[::16] + np.float32(0.0)
            own.append(decode(q).astype(BF))
            score = np.take_along_axis(s, base[r].reshape(8, -1), axis=1).reshape(8, M, 2 * h)
            o = np.argsort(-score, axis=2, kind="stable")
            b, e = np.take_along_axis(base[r], o, axis=2), np.take_along_axis(top[r], o, axis=2)
            np.put_along_axis(up[r], e[:, :, :h].reshape(8, -1), np.roll(b[:, :, h:], 1, axis=1).reshape(8, -1), axis=1)
            base[r], top[r] = b[:, :, :h], np.roll(e[:, :, h:], 1, axis=1)
            np.put_along_axis(up[r], top[r].reshape(8, -1), np.stack([C + np.arange(M * h)] * 8), axis=1)
            a = gcols(own[r], top[r].reshape(8, -1)).astype(np.float32) + gcols(own[r], base[r].reshape(8, -1)).astype(np.float32)
            ends.append(mx_ref.quantize(np.ascontiguousarray((a * np.float32(0.5)).astype(BF))))
        for r in range(N):
            made = tile([mx_ref.matmul(pick(lay[r], np.arange(128 * b, 128 * b + 128)), ends[r - 1]) * np.float32(0.03125) for b in range(4)])
            near = gcols(np.concatenate([own[r], made], axis=1), up[r]).astype(np.float32)
            now[r] = ((own[r].astype(np.float32) + near) * np.float32(0.5)).astype(BF)
    y, op = np.zeros((N, 128, C), np.float32), np.zeros((N, 8, C), np.float32)
    oc, osc = np.zeros((N, 128, 4 * C), np.uint8), np.zeros((N, 16, C), np.uint8)
    for r in range(N):
        q = mx_ref.quantize(now[r])
        y[r] = mx_ref.matmul(mx_ref.quantize(v[r]), q)
        op[r] = up[r]
        oc[r], osc[r] = emit(q)
    return {"y": y, "op": op, "oc": oc, "osc": osc}

@@ -1,0 +1,381 @@
+import numpy as np
+from concourse.mybir import dt, AluOpType, ActivationFunctionType
+
+Op = AluOpType
+COPY = ActivationFunctionType.Copy
+ROUNDS, PLACES = 3, 256
+LANES = [16, 8, 4]
+COUNT = [16 * n for n in LANES]
+TINY = 1e-37
+HUGE = 1e28
+LATE = [True, False, False]
+ONV = [[2, 3], [3], [3]]
+
+SCRATCH = {
+    "ut": ("sbuf", [128, 512], "bfloat16"), "vt": ("sbuf", [128, 512], "bfloat16"), "twi": ("sbuf", [128, 16], "int32"),
+    "twt": ("sbuf", [128, 16], "uint16"),
+    "wq": ("sbuf", [128, 512], "float8_e4m3fn_x4"), "wsc": ("sbuf", [128, 512], "uint8"),
+    "qu": ("sbuf", [128, 128], "float8_e4m3fn_x4"), "su": ("sbuf", [128, 128], "uint8"),
+    "qur": ("sbuf", [128, 128], "float8_e4m3fn_x4"), "sur": ("sbuf", [128, 128], "uint8"),
+    "qv": ("sbuf", [128, 128], "float8_e4m3fn_x4"), "sv": ("sbuf", [128, 128], "uint8"),
+    "cz": ("sbuf", [128, 2048], "bfloat16"), "half": ("sbuf", [128, 128], "bfloat16"), "idn": ("sbuf", [128, 128], "bfloat16"),
+    "qc": ("sbuf", [128, 512], "float8_e4m3fn_x4"), "scc": ("sbuf", [128, 512], "uint8"),
+    "ib": ("sbuf", [128, 96], "int32"), "ibm": ("sbuf", [128, 96], "int32"),
+    "ibd": ("sbuf", [128, 272], "int32"), "ibe": ("sbuf", [128, 272], "int32"),
+    "win": ("sbuf", [128, 64], "bfloat16"), "kapu": ("sbuf", [128, 16], "uint16"),
+    "rept": ("sbuf", [128, 16], "uint16"), "upl": ("sbuf", [128, 8], "uint16"), "lnk": ("sbuf", [128, 17], "uint16"),
+    "colv": ("sbuf", [128, 1], "float32"), "i16": ("sbuf", [128, 17], "float32"),
+    "r16": ("sbuf", [128, 256], "bfloat16"), "rs": ("sbuf", [128, 256], "bfloat16"),
+    "dg1": ("sbuf", [128, 256], "float32"), "dg2": ("sbuf", [128, 272], "float32"),
+    "m16": ("sbuf", [128, 48], "float32"), "mc": ("sbuf", [128, 16], "float32"), "msh": ("sbuf", [128, 64], "int32"),
+    "mdf": ("sbuf", [128, 32], "float32"), "mdg": ("sbuf", [128, 32], "float32"),
+    "upi": ("sbuf", [128, 1], "int32"), "upc": ("sbuf", [128, 1], "float32"), "loc": ("sbuf", [128, 1], "float32"),
+    "win2": ("sbuf", [128, 512], "float32"),
+    "sco": ("sbuf", [128, 256], "float32"), "km": ("sbuf", [128, 272], "float32"), "uu": ("sbuf", [128, 272], "float32"),
+    "ks": ("sbuf", [128, 256], "float32"), "dd": ("sbuf", [128, 256], "float32"),
+    "cmp": ("sbuf", [128, 256], "bfloat16"), "pos": ("sbuf", [128, 256], "bfloat16"),
+    "sel": ("sbuf", [128, 256], "bfloat16"), "ses": ("sbuf", [128, 256], "bfloat16"),
+    "sel2": ("sbuf", [128, 128], "bfloat16"), "ses2": ("sbuf", [128, 128], "bfloat16"),
+    "ef": ("sbuf", [128, 16], "float32"), "et": ("sbuf", [128, 16], "uint16"), "post": ("sbuf", [128, 16], "uint16"),
+    "vwx": ("sbuf", [128, 272], "float32"), "ur": ("sbuf", [128, 256], "float32"), "um": ("sbuf", [128, 256], "float32"),
+    "us": ("sbuf", [128, 256], "float32"), "urow": ("sbuf", [128, 256], "float32"),
+    "bta": ("sbuf", [128, 128], "bfloat16"), "btb": ("sbuf", [128, 128], "bfloat16"), "bt0": ("sbuf", [128, 256], "bfloat16"),
+    "bt1": ("sbuf", [128, 128], "bfloat16"), "bt2": ("sbuf", [128, 64], "bfloat16"),
+    "fp": ("sbuf", [128, 1024], "bfloat16"), "fe": ("sbuf", [128, 4 * 272], "bfloat16"), "f0": ("sbuf", [128, 256], "bfloat16"),
+    "vw": ("sbuf", [128, 4 * 384], "bfloat16"), "nr": ("sbuf", [128, 1024], "bfloat16"), "ysb": ("sbuf", [128, 256], "float32"),
+    "pf": ("psum", [128, 2048], "float32"), "pg": ("psum", [128, 2048], "float32"),
+}
+for _t in range(4):
+    SCRATCH["xt%d" % _t] = ("sbuf", [128, 1024], "bfloat16")
+    SCRATCH["qx%d" % _t] = ("sbuf", [128, 256], "float8_e4m3fn_x4")
+    SCRATCH["sx%d" % _t] = ("sbuf", [128, 256], "uint8")
+    if _t:
+        SCRATCH["upt%d" % _t] = ("sbuf", [128, 16], "uint16")
+for _t in range(3):
+    _c = COUNT[_t] // 16
+    SCRATCH["lqx%d" % _t] = ("sbuf", [128, 256], "float8_e4m3fn_x4")
+    SCRATCH["lsx%d" % _t] = ("sbuf", [128, 256], "uint8")
+    SCRATCH["ct%d" % _t] = ("sbuf", [128, _c + 1], "uint16")
+    SCRATCH["lct%d" % _t] = ("sbuf", [128, _c + 1], "uint16")
+    SCRATCH["cn%d" % _t] = ("sbuf", [128, COUNT[_t] + 16], "float32")
+    SCRATCH["mx%d" % _t] = ("sbuf", [128, COUNT[_t]], "float32")
+    SCRATCH["et%d" % _t] = ("sbuf", [128, 512], "bfloat16")
+    SCRATCH["qe%d" % _t] = ("sbuf", [128, 128], "float8_e4m3fn_x4")
+    SCRATCH["se%d" % _t] = ("sbuf", [128, 128], "uint8")
+    if _t:
+        SCRATCH["ctr%d" % _t] = ("sbuf", [128, COUNT[_t - 1] + 16], "bfloat16")
+        SCRATCH["cb%d" % _t] = ("sbuf", [128, _c + 1], "uint16")
+
+SEMAPHORES = (["v", "s", "p", "gq", "lx", "lu", "lt", "lw", "lws", "lv", "snt", "oa", "ob", "oo"]
+              + ["ax%d" % t for t in range(3)] + ["al%d" % t for t in range(3)])
+
+
+def rank_program(g, core, T, topo):
+    rank = T.rank_of(core)
+    if rank is None:
+        return
+    cores = T.cores
+    nxt, prv = cores[(rank + 1) % len(cores)], cores[(rank - 1) % len(cores)]
+    n_in, n_out = len(topo.engines(prv, core)), len(topo.engines(core, nxt))
+    rid, pid = topo.addr(nxt)[0], topo.addr(nxt)[1]
+
+    eng = {"g": g, "v": g.vector, "s": g.scalar, "p": g.tensor, "y": g.sync}
+    own = {"g": "gq", "v": "v", "s": "s", "p": "p"}
+    count, waited = {}, {}
+    known = {q: {} for q in eng}
+    writer, readers = {}, {}
+
+    def need(q, toks):
+        for sem, val, clock in sorted(toks, key=lambda k: -len(k[2])):
+            if known[q].get(sem, 0) >= val:
+                continue
+            best = max(v for s, v, c in toks if s == sem)
+            eng[q].wait_ge(T.sem[sem], best)
+            waited[sem] = max(waited.get(sem, 0), best)
+            for s, v, c in toks:
+                if s == sem:
+                    for a in c:
+                        known[q][a] = max(known[q].get(a, 0), c[a])
+            known[q][sem] = max(known[q].get(sem, 0), best)
+
+    def deps(q, reads, writes):
+        toks = [writer[k] for k in reads if k in writer]
+        for k in writes:
+            if k in writer:
+                toks.append(writer[k])
+            toks += readers.get(k, [])
+        need(q, toks)
+
+    def op(q, call, reads, writes, sem=None, inc=1):
+        deps(q, reads, writes)
+        sem = sem or own[q]
+        count[sem] = count.get(sem, 0) + inc
+        call().then_inc(T.sem[sem], inc)
+        tok = (sem, count[sem], dict(known[q]))
+        for k in reads:
+            readers.setdefault(k, []).append(tok)
+        for k in writes:
+            writer[k] = tok
+            readers[k] = []
+
+    V, S, P, Y = g.vector, g.scalar, g.tensor, g.sync
+
+    def send(out_ap, in_ap, sem, reads):
+        deps("g", reads, [])
+        g.remote_dma(out_ap=out_ap, in_ap=in_ap, remote_sem=T.sem[sem], local_sem=T.sem.snt, pid=pid, routing_id=rid,
+                     dma_engine_mask=topo.mask(core, nxt))
+        count["snt"] = count.get("snt", 0) + n_out
+
+    def arrive(sem, times, keys):
+        count[sem] = times * n_in
+        for k in keys:
+            writer[k] = (sem, times * n_in, {})
+
+    op("y", lambda: Y.dma_start(T.xt0[:, :], T.x[:, :]), [], ["xt0"], "lx", 16)
+    op("s", lambda: S.dma_start(T.ut[:, :], T.u[:, :]), [], ["ut"], "lu", 16)
+    op("s", lambda: S.dma_start(T.twi[:, :], T.tw[:, :]), [], ["twi"], "lt", 16)
+    deps("y", ["xt0"], [])
+    op("y", lambda: Y.dma_start(T.wq[:, 0:512].bitcast(dt.uint8), T.wc[:, 0:2048]), [], ["wq"], "lw", 16)
+    op("y", lambda: Y.dma_start(T.wsc[:, 0:512], T.ws[:, 0:512]), [], ["wsc"], "lws", 16)
+    op("y", lambda: Y.dma_start(T.vt[:, :], T.v[:, :]), [], ["vt"], "lv", 16)
+
+    op("v", lambda: V.memset(T.half[:, :], 0.5), [], ["half"])
+    op("v", lambda: V.memset(T.cz[:, :], 0.0), [], ["cz"])
+    op("g", lambda: g.affine_select(T.idn[:, :], T.half[:, :], [[-1, 128]], Op.is_equal, 0.0, 0, 1), ["half"], ["idn"])
+    op("g", lambda: g.iota(T.i16[:, :], [[16, 17]], 0, 0, allow_small_or_imprecise_dtypes=True), [], ["i16"])
+    for a, (pat, base, mul) in enumerate([([[16, 1], [1, 2], [2, 8]], 0, -1), ([[8, 2], [1, 2], [2, 4]], 0, -1),
+                                          ([[4, 4], [1, 2], [2, 2]], 0, -1), ([[1, 16]], 0, -1),
+                                          ([[0, 16]], 0, 1), ([[1, 16]], 0, 0)]):
+        op("g", lambda: g.iota(T.ib[:, 16 * a:16 * a + 16], pat, base, mul), [], ["ib%d" % a])
+    op("g", lambda: g.iota(T.r16[:, :], [[0, 16], [1, 16]], 0, 0, allow_small_or_imprecise_dtypes=True), [], ["r16"])
+    op("g", lambda: g.iota(T.win2[:, 0:256], [[1, 256]], 0, 0, allow_small_or_imprecise_dtypes=True), [], ["ramp"])
+    op("g", lambda: g.iota(T.ibd[:, :], [[-1, 136], [0, 2]], 8, 1), [], ["ibd"])
+
+    for b in range(4):
+        op("s", lambda: S.activation(T.cz[:, 512 * b + b:512 * b + 512:4], T.idn[:, :], COPY), ["idn", "cz"], ["cz%d" % b])
+    op("v", lambda: V.tensor_scalar(T.upl[:, :], T.i16[:, 0:8], 1.0, None, Op.mult), ["i16"], ["upl"])
+    op("v", lambda: V.tensor_scalar(T.rept[:, :], T.i16[:, 0:16], 15.0, None, Op.add), ["i16"], ["rept"])
+    op("v", lambda: V.tensor_scalar(T.ibm[:, :], T.ib[:, :], 15, None, Op.bitwise_and), ["ib%d" % a for a in range(6)], ["ibm"])
+    op("v", lambda: V.tensor_scalar(T.win[:, :], T.ibm[:, 0:64], 0.0, None, Op.is_equal), ["ibm"], ["win"])
+    op("v", lambda: V.tensor_copy(T.kapu[:, :], T.ibm[:, 64:80]), ["ibm"], ["kapu"])
+    op("v", lambda: V.tensor_tensor(T.mc[:, :], T.ibm[:, 80:96], T.ibm[:, 64:80], Op.is_lt), ["ibm"], ["mc"])
+    op("s", lambda: S.activation(T.dg1[:, :], T.win[:, 48:64].indirect(T.kapu[:, 0:16]), COPY), ["win", "kapu"], ["dg1"])
+    op("v", lambda: V.tensor_scalar(T.m16[:, 0:16], T.mc[:, :], TINY, None, Op.mult), ["mc"], ["m160"])
+    op("v", lambda: V.tensor_scalar(T.rs[:, :], T.r16[:, :], 1.0, None, Op.min), ["r16"], ["rs"])
+    op("v", lambda: V.quantize_mx(T.qc[:, 0:512], T.scc[:, 0:512], T.cz[:, 0:2048]), ["cz0", "cz1", "cz2", "cz3"], ["qc", "scc"])
+    op("v", lambda: V.quantize_mx(T.qu[:, 0:128], T.su[:, 0:128], T.ut[:, 0:512]), ["ut"], ["qu", "su"])
+    op("v", lambda: V.tensor_copy(T.qur[:, 0:128].bitcast(dt.uint32), T.qu[:, 0:128].bitcast(dt.uint32).indirect(T.upl[:, 0:8])),
+       ["qu", "upl"], ["qur"])
+    op("s", lambda: S.activation(T.sur[:, 0:128], T.su[:, 0:128].indirect(T.upl[:, 0:8]), COPY), ["su", "upl"], ["sur"])
+    op("v", lambda: V.tensor_copy(T.twt[:, :], T.twi[:, :]), ["twi"], ["twt"])
+
+    def later():
+        for a in (1, 2):
+            c = 32 * (a - 1)
+            op("v", lambda: V.tensor_scalar(T.msh[:, c:c + 32], T.ibm[:, 64:96], 4 - a, None, Op.arith_shift_right), ["ibm"], ["msh%d" % a])
+        op("v", lambda: V.tensor_scalar(T.upi[:, :], T.ibm[:, 64:65], 1, None, Op.bitwise_and), ["ibm"], ["upi"])
+        op("v", lambda: V.tensor_scalar(T.colv[:, :], T.ibm[:, 64:65], 7.5, 2.0, Op.max, Op.mult), ["ibm"], ["colv"])
+        for a in (1, 2):
+            c, m = 32 * (a - 1), 16 * (a - 1)
+            op("v", lambda: V.tensor_tensor(T.mdf[:, m:m + 16], T.msh[:, c:c + 16], T.msh[:, c + 16:c + 32], Op.subtract), ["msh%d" % a], ["mdf%d" % a])
+        op("v", lambda: V.tensor_copy(T.upc[:, :], T.upi[:, :]), ["upi"], ["upc"])
+        op("v", lambda: V.tensor_scalar(T.loc[:, :], T.upi[:, :], -1.0, 1.0, Op.mult, Op.add), ["upi"], ["loc"])
+        op("v", lambda: V.tensor_scalar(T.lnk[:, :], T.i16[:, :], T.colv[:, 0:1], 15.0, Op.add, Op.subtract), ["i16", "colv"], ["lnk"])
+        op("v", lambda: V.tensor_scalar(T.mdg[:, :], T.mdf[:, :], HUGE, None, Op.mult), ["mdf1", "mdf2"], ["mdg"])
+        for a in (1, 2):
+            m = 16 * (a - 1)
+            op("v", lambda: V.tensor_tensor(T.m16[:, 16 * a:16 * a + 16], T.mdg[:, m:m + 16], T.m16[:, 0:16], Op.add), ["mdg", "m160"], ["m16%d" % a])
+
+    def later2():
+        for a in (1, 2):
+            op("v", lambda: V.memset(T["et%d" % a][:, :], 0.0), [], ["et%d.%d" % (a, b) for b in range(4)])
+        op("v", lambda: V.tensor_scalar(T.ibe[:, :], T.ibd[:, :], 15, None, Op.bitwise_and), ["ibd"], ["ibe"])
+        op("v", lambda: V.tensor_scalar(T.dg2[:, :], T.ibe[:, :], 0.0, None, Op.is_equal), ["ibe"], ["dg2"])
+        op("v", lambda: V.quantize_mx(T.qv[:, 0:128], T.sv[:, 0:128], T.vt[:, 0:512]), ["vt"], ["qv", "sv"])
+
+    def slots(t):
+        L, h, cn = LANES[t], LANES[t] // 2, T["cn%d" % t]
+        A = 16 + 16 // L
+        k = "cn%d" % t
+        op("g", lambda: g.iota(cn[:, :], [[h, A], [1, L]], PLACES + h * (1 - 16 // L), 0, allow_small_or_imprecise_dtypes=True), [], [k])
+        op("g", lambda: g.affine_select(cn[:, :], cn[:, :], [[0, A], [-1, L]], Op.is_ge, 0.0, h - 1, 0), [k], [k])
+        op("g", lambda: g.iota(cn[:, L * (A - 1):L * (A - 1) + h], [[1, h]], PLACES, 0, allow_small_or_imprecise_dtypes=True), [k], [k])
+
+    for t in range(ROUNDS):
+        L, h, N = LANES[t], LANES[t] // 2, COUNT[t]
+        C, M = N // 16, N // 2
+        qx, sx, xt = T["qx%d" % t], T["sx%d" % t], T["xt%d" % t]
+        kq, ksx = "qx%d" % t, "sx%d" % t
+        ct, lct, mx, bt = T["ct%d" % t], T["lct%d" % t], T["mx%d" % t], T["bt%d" % t]
+        kct, kbt = "ct%d" % t, "bt%d" % t
+        xk = ["xt0"] if t == 0 else ["xt%d.%d" % (t, b) for b in range(4)]
+        op("v", lambda: V.quantize_mx(qx[:, 0:256], sx[:, 0:256], xt[:, 0:1024]), xk, [kq, ksx])
+        for a in range(2):
+            op("p", lambda: P.matmul_mx(T.pg[:, 512 * a:512 * a + 128], T.qur[:, 0:128], T.sur[:, 0:128],
+                                        qx[:, 128 * a:128 * a + 128], sx[:, 128 * a:128 * a + 128], True, True),
+               ["qur", "sur", kq, ksx], ["pg%d" % a])
+        send(T["lqx%d" % t][:, 0:256].bitcast(dt.uint8), qx[:, 0:256].bitcast(dt.uint8), "ax%d" % t, [kq])
+        send(T["lsx%d" % t][:, 0:256], sx[:, 0:256], "ax%d" % t, [ksx])
+        if t == 0:
+            slots(0)
+        op("v", lambda: V.tensor_copy(T.sco[:, 0:128], T.pg[:, 0:128]), ["pg0"], ["sco0"])
+        op("s", lambda: S.activation(T.sco[:, 128:256], T.pg[:, 512:640], COPY), ["pg1"], ["sco1"])
+        if t == 0:
+            lst, w, kl, lo, st, dg, kd = T.twt[:, 0:16], 256, "twt", 0, 1, T.dg1, "dg1"
+        else:
+            w, lo, st, dg, kd = COUNT[t - 1] + 16, 16, 2, T.dg2, "dg2"
+            lst, kl = T["ct%d" % (t - 1)][:, 0:w // 16], "ct%d" % (t - 1)
+        hi = lo + st * N
+        op("v", lambda: V.tensor_tensor(T.km[:, 0:w], T.sco[:, 0:256].indirect(lst), dg[:, 0:w], Op.mult), ["sco0", "sco1", kl, kd], ["km"])
+        op("s", lambda: S.activation(T.uu[:, 0:w], T.sco[:, 0:256].indirect(lst), COPY), ["sco0", "sco1", kl], ["uu"])
+        if t == 0:
+            op("s", lambda: S.activation(T.mx0[:, :], T.m16[:, 0:16].indirect(T.kapu[:, 0:16]), COPY), ["m160", "kapu"], ["mx0"])
+            op("s", lambda: S.activation(T.bt0[:, :], T.win2[:, 0:256].indirect(T.twt[:, 0:16]), COPY), ["ramp", "twt"], ["bt0"])
+        op("v", lambda: V.tensor_tensor_scan(T.ks[:, 0:N], T.rs[:, 0:N], T.km[:, lo:hi:st], 0.0, Op.mult, Op.add), ["rs", "km"], ["ks"])
+        op("v", lambda: V.tensor_tensor(T.dd[:, 0:N], T.ks[:, 0:N].indirect(T.rept[:, 0:C]), T.uu[:, lo:hi:st], Op.subtract), ["ks", "rept", "uu"], ["dd"])
+        op("v", lambda: V.tensor_tensor(T.cmp[:, 0:N], T.dd[:, 0:N], mx[:, :], Op.is_lt), ["dd", "mx%d" % t], ["cmp"])
+        op("v", lambda: V.tensor_tensor_scan(T.pos[:, 0:N], T.rs[:, 0:N], T.cmp[:, 0:N], 0.0, Op.mult, Op.add), ["rs", "cmp"], ["pos"])
+        op("v", lambda: V.tensor_copy(T.post[:, 0:C], T.pos[:, 15:N:16]), ["pos"], ["post"])
+        op("v", lambda: V.tensor_tensor(T.sel[:, 0:N], T.win[:, 16 * t:16 * t + 16].indirect(T.post[:, 0:C]), bt[:, :], Op.mult), ["win", "post", kbt], ["sel"])
+        op("v", lambda: V.tensor_tensor_scan(T.ses[:, 0:N], T.rs[:, 0:N], T.sel[:, 0:N], 0.0, Op.mult, Op.add), ["rs", "sel"], ["ses"])
+        op("v", lambda: V.tensor_copy(ct[:, 1:C + 1], T.ses[:, 15:N:16]), ["ses"], [kct + "a"])
+        op("v", lambda: V.tensor_copy(ct[:, 0:1], T.ses[:, N - 1:N]), ["ses"], [kct])
+        send(lct[:, :], ct[:, :], "al%d" % t, [kct + "a", kct])
+        if t == 0:
+            slots(1)
+            slots(2)
+
+        for b in range(4):
+            op("p", lambda: P.matmul_mx(T.pf[:, 512 * b:512 * b + 256], T.qc[:, 128 * b:128 * b + 128], T.scc[:, 128 * b:128 * b + 128],
+                                        qx[:, 0:256], sx[:, 0:256], True, True), ["qc", "scc", kq, ksx], ["pf%d" % b])
+
+        def window(b):
+            op("s", lambda: S.activation(T.vw[:, 384 * b:384 * b + 256], T.pf[:, 512 * b:512 * b + 256], COPY), ["pf%d" % b], ["vwf%d" % b])
+        for b in (0, 1, 2):
+            window(b)
+        if t == 0:
+            later()
+
+        arrive("ax%d" % t, 2, ["lqx%d" % t])
+
+        def arrived(b, q):
+            dst, src = T.fp[:, 256 * b:256 * b + 256], T.pg[:, 512 * b:512 * b + 256]
+            op(q, lambda: V.tensor_copy(dst, src) if q == "v" else S.activation(dst, src, COPY), ["pg%d" % b], ["fp%d" % b])
+        for b in range(4):
+            op("p", lambda: P.matmul_mx(T.pg[:, 512 * b:512 * b + 256], T.qc[:, 128 * b:128 * b + 128], T.scc[:, 128 * b:128 * b + 128],
+                                        T["lqx%d" % t][:, 0:256], T["lsx%d" % t][:, 0:256], True, True), ["qc", "scc", "lqx%d" % t], ["pg%d" % b])
+        on_s = [b for b in range(4) if b not in ONV[t]]
+        op("v", lambda: V.tensor_tensor(T.ef[:, 0:C], T.pos[:, 15:N:16], T.i16[:, 0:C], Op.add), ["pos", "i16"], ["ef"])
+        if t < ROUNDS - 1:
+            ctr, kr = T["ctr%d" % (t + 1)], "ctr%d" % (t + 1)
+            op("s", lambda: S.activation(ctr[:, :], T.win2[:, 0:256].indirect(ct[:, 0:C + 1]), COPY), ["ramp", kct + "a", kct], [kr])
+            op("s", lambda: S.activation(T.bta[:, 0:M], ctr[:, 16:16 + N:2], COPY, scale=T.loc[:, 0:1]), [kr, "loc"], ["bta"])
+            op("s", lambda: S.activation(T.btb[:, 0:M], ctr[:, 17 - L:17 - L + N:2], COPY, scale=T.upc[:, 0:1]), [kr, "upc"], ["btb"])
+        if t:
+            arrived(on_s[0], "s")
+            cb, brow = T["cb%d" % t], T["ctr%d" % t][:, 16:16 + 2 * N:2]
+            op("v", lambda: V.tensor_tensor(T.sel2[:, 0:N], T.win[:, 48:64].indirect(T.post[:, 0:C]), brow, Op.mult), ["win", "post", "ctr%d" % t], ["sel2"])
+            op("v", lambda: V.tensor_scalar(T.et[:, 0:C], T.ef[:, 0:C], float(16 - h), None, Op.add), ["ef"], ["et"])
+            op("v", lambda: V.tensor_tensor_scan(T.ses2[:, 0:N], T.rs[:, 0:N], T.sel2[:, 0:N], 0.0, Op.mult, Op.add), ["rs", "sel2"], ["ses2"])
+            op("v", lambda: V.tensor_copy(cb[:, 1:C + 1], T.ses2[:, 15:N:16]), ["ses2"], ["cba"])
+            op("v", lambda: V.tensor_copy(cb[:, 0:1], T.ses2[:, N - 1:N]), ["ses2"], ["cb"])
+            op("v", lambda: V.tensor_tensor(T.vwx[:, 0:N + 16], T.win2[:, 0:256].indirect(cb[:, 0:C + 1]), T["cn%d" % t][:, :], Op.max),
+               ["ramp", "cba", "cb", "cn%d" % t], ["vwx"])
+        else:
+            op("v", lambda: V.tensor_scalar(T.et[:, 0:C], T.ef[:, 0:C], float(16 - h), None, Op.add), ["ef"], ["et"])
+            op("v", lambda: V.tensor_tensor(T.vwx[:, 0:N + 16], ctr[:, :].indirect(T.lnk[:, 0:C + 1]), T.cn0[:, :], Op.max), [kr, "lnk", "cn0"], ["vwx"])
+        op("s", lambda: S.activation(T.win2[:, 256:256 + N], T.vwx[:, 0:N + 16].indirect(T.et[:, 0:C]), COPY), ["vwx", "et"], ["val"])
+        if t == 0:
+            for a in (1, 2):
+                op("s", lambda: S.activation(T["mx%d" % a][:, :], T.m16[:, 16 * a:16 * a + 16].indirect(T.kapu[:, 0:COUNT[a] // 16]), COPY),
+                   ["m16%d" % a, "kapu"], ["mx%d" % a])
+            arrived(on_s[0], "s")
+        for b in on_s[1:]:
+            arrived(b, "s")
+        if t < ROUNDS - 1:
+            op("v", lambda: V.tensor_tensor(T["bt%d" % (t + 1)][:, :], T.bta[:, 0:M], T.btb[:, 0:M], Op.add), ["bta", "btb"], ["bt%d" % (t + 1)])
+        upt = T["upt%d" % (t + 1)]
+        if t == 0:
+            later2()
+        else:
+            for b in ONV[t]:
+                arrived(b, "v")
+
+        def table():
+            if t == 0:
+                op("v", lambda: V.tensor_tensor(T.um[:, :], T.ur[:, :], T.dg1[:, :], Op.mult), ["ur", "dg1"], ["um"])
+            op("v", lambda: V.tensor_tensor_scan(T.us[:, :], T.rs[:, :], T.um[:, :], 0.0, Op.mult, Op.add), ["rs", "um"], ["us"])
+            op("v", lambda: V.tensor_copy(upt[:, :], T.us[:, 15:256:16]), ["us"], ["upt%d" % (t + 1)])
+        if t == 0:
+            op("v", lambda: V.tensor_copy(T.ur[:, 0:256].indirect(T.twt[:, 0:16]), T.win2[:, 256:512]), ["val", "twt"], ["ur"])
+            if not LATE[0]:
+                table()
+            for b in ONV[t]:
+                arrived(b, "v")
+        else:
+            op("v", lambda: V.tensor_tensor(T.um[:, :], T.win2[:, 0:256 + N].indirect(T["upt%d" % t][:, 0:16]), T.dg1[:, :], Op.mult),
+               ["ramp", "val", "upt%d" % t, "dg1"], ["um"])
+            if not LATE[t]:
+                table()
+
+        arrive("al%d" % t, 1, ["lct%d" % t])
+        ee, ke = T["et%d" % t], "et%d" % t
+        W = N + 16
+
+        def ends(q, b):
+            src = T.fp[:, 256 * b:256 * b + 256].indirect(lct[:, 0:C + 1])
+            dst = T.fe[:, 272 * b:272 * b + W]
+            op(q, lambda: V.tensor_copy(dst, src) if q == "v" else S.activation(dst, src, COPY), ["fp%d" % b, "lct%d" % t], ["fe%d" % b])
+
+        def mean(b):
+            op("v", lambda: V.tensor_tensor(ee[:, b:4 * M:4], T.fe[:, 272 * b + 16:272 * b + 16 + N:2],
+                                            T.fe[:, 272 * b + 17 - L:272 * b + 17 - L + N:2], Op.add), ["fe%d" % b], [ke + ".%d" % b])
+        own_b = ONV[t][-1]
+        order = [b for b in range(4) if b != own_b]
+        ends("v", own_b)
+        for b in order:
+            ends("s", b)
+        mean(own_b)
+        for b in order:
+            mean(b)
+        window(3)
+        op("s", lambda: S.activation(T.f0[:, :], T.pf[:, 0:256], COPY), ["pf0"], ["f0"])
+        qe, se, kqe = T["qe%d" % t], T["se%d" % t], "qe%d" % t
+        op("v", lambda: V.quantize_mx(qe[:, 0:128], se[:, 0:128], ee[:, 0:512]), [ke + ".%d" % b for b in range(4)], [kqe])
+        for b in (1, 0, 2, 3):
+            op("p", lambda: P.matmul_mx(T.pg[:, 512 * b:512 * b + 128], T.wq[:, 128 * b:128 * b + 128], T.wsc[:, 128 * b:128 * b + 128],
+                                        qe[:, 0:128], se[:, 0:128], True, True), ["wq", "wsc", kqe], ["pg%d" % b])
+        if LATE[t]:
+            table()
+        xn = T["xt%d" % (t + 1)]
+        kup = "upt%d" % (t + 1)
+        for b in (1, 0, 2, 3):
+            op("v", lambda: V.tensor_scalar(T.vw[:, 384 * b + 256:384 * b + 256 + M], T.pg[:, 512 * b:512 * b + M], 0.015625, None, Op.mult),
+               ["pg%d" % b], ["vwh%d" % b])
+        for b in (1, 2, 3):
+            op("s", lambda: S.activation(T.nr[:, 256 * b:256 * b + 256], T.vw[:, 384 * b:384 * b + 256 + M].indirect(upt[:, 0:16]), COPY),
+               ["vwf%d" % b, "vwh%d" % b, kup], ["nr%d" % b])
+        op("v", lambda: V.tensor_tensor(xn[:, 0:1024:4], T.vw[:, 0:256 + M].indirect(upt[:, 0:16]), T.f0[:, :], Op.add),
+           ["vwf0", "vwh0", "f0", kup], ["xt%d.0" % (t + 1)])
+        for b in (1, 2, 3):
+            op("v", lambda: V.tensor_tensor(xn[:, b:1024:4], T.pf[:, 512 * b:512 * b + 256], T.nr[:, 256 * b:256 * b + 256], Op.add),
+               ["pf%d" % b, "nr%d" % b], ["xt%d.%d" % (t + 1, b)])
+        if t == ROUNDS - 1:
+            op("v", lambda: V.quantize_mx(T.qx3[:, 0:256], T.sx3[:, 0:256], xn[:, 0:1024]), ["xt3.%d" % b for b in range(4)], ["qx3", "sx3"])
+            op("s", lambda: S.activation(T.urow[:, :], T.win2[:, 0:256 + N].indirect(T["upt%d" % t][:, 0:16]), COPY), ["ramp", "val", "upt%d" % t], ["urow"])
+            op("y", lambda: Y.dma_start(T.op[:, :], T.urow[0:128:16, :]), ["urow"], [], "oo", 16)
+
+    for a in range(2):
+        op("p", lambda: P.matmul_mx(T.pg[:, 512 * a:512 * a + 128], T.qv[:, 0:128], T.sv[:, 0:128],
+                                    T.qx3[:, 128 * a:128 * a + 128], T.sx3[:, 128 * a:128 * a + 128], True, True), ["qv", "sv", "qx3", "sx3"], ["pg%d" % a])
+    op("y", lambda: Y.dma_start(T.oc[:, 0:1024], T.qx3[:, 0:256].bitcast(dt.uint8)), ["qx3"], [], "oa", 16)
+    for k in range(4):
+        op("y", lambda: Y.dma_start(T.osc[4 * k:4 * k + 4, 0:256], T.sx3[32 * k:32 * k + 4, 0:256]), ["sx3"], [], "oa", 16)
+    op("v", lambda: V.tensor_copy(T.ysb[:, 0:128], T.pg[:, 0:128]), ["pg0"], ["ya"])
+    op("s", lambda: S.activation(T.ysb[:, 128:256], T.pg[:, 512:640], COPY), ["pg1"], ["yb"])
+    op("s", lambda: S.dma_start(T.y[:, 0:128], T.ysb[:, 0:128]), ["ya"], [], "ob", 16)
+    op("s", lambda: S.dma_start(T.y[:, 128:256], T.ysb[:, 128:256]), ["yb"], [], "ob", 16)
+
+    for sem in count:
+        if waited.get(sem, 0) < count[sem]:
+            g.wait_ge(T.sem[sem], count[sem])

@@ -8,7 +8,6 @@ LANES = [16, 8, 4]
 COUNT = [16 * n for n in LANES]
 TINY = 1e-37
 HUGE = 1e28
-LATE = [True, False, False]
 ONV = [[2, 3], [3], [3]]
 
 SCRATCH = {
@@ -76,7 +75,12 @@ def rank_program(g, core, T, topo):
         return
     cores = T.cores
     nxt, prv = cores[(rank + 1) % len(cores)], cores[(rank - 1) % len(cores)]
-    n_in, n_out = len(topo.engines(prv, core)), len(topo.engines(core, nxt))
+
+    def shares(a, b):
+        e = topo.engines(a, b)
+        return (e[:8], e[8:]) if len(e) > 8 else (e, e)
+    codes_by, scales_by = shares(core, nxt)
+    n_list, n_state = len(topo.engines(prv, core)), sum(len(e) for e in shares(prv, core))
     rid, pid = topo.addr(nxt)[0], topo.addr(nxt)[1]
 
     eng = {"g": g, "v": g.vector, "s": g.scalar, "p": g.tensor, "y": g.sync}
@@ -120,16 +124,16 @@ def rank_program(g, core, T, topo):
 
     V, S, P, Y = g.vector, g.scalar, g.tensor, g.sync
 
-    def send(out_ap, in_ap, sem, reads):
+    def send(out_ap, in_ap, sem, reads, by):
         deps("g", reads, [])
         g.remote_dma(out_ap=out_ap, in_ap=in_ap, remote_sem=T.sem[sem], local_sem=T.sem.snt, pid=pid, routing_id=rid,
-                     dma_engine_mask=topo.mask(core, nxt))
-        count["snt"] = count.get("snt", 0) + n_out
+                     dma_engine_mask=sum(1 << e for e in by))
+        count["snt"] = count.get("snt", 0) + len(by)
 
-    def arrive(sem, times, keys):
-        count[sem] = times * n_in
+    def arrive(sem, n, keys):
+        count[sem] = n
         for k in keys:
-            writer[k] = (sem, times * n_in, {})
+            writer[k] = (sem, n, {})
 
     op("y", lambda: Y.dma_start(T.xt0[:, :], T.x[:, :]), [], ["xt0"], "lx", 16)
     op("s", lambda: S.dma_start(T.ut[:, :], T.u[:, :]), [], ["ut"], "lu", 16)
@@ -162,7 +166,6 @@ def rank_program(g, core, T, topo):
     op("s", lambda: S.activation(T.dg1[:, :], T.win[:, 48:64].indirect(T.kapu[:, 0:16]), COPY), ["win", "kapu"], ["dg1"])
     op("v", lambda: V.tensor_scalar(T.m16[:, 0:16], T.mc[:, :], TINY, None, Op.mult), ["mc"], ["m160"])
     op("v", lambda: V.tensor_scalar(T.rs[:, :], T.r16[:, :], 1.0, None, Op.min), ["r16"], ["rs"])
-    op("v", lambda: V.quantize_mx(T.qc[:, 0:512], T.scc[:, 0:512], T.cz[:, 0:2048]), ["cz0", "cz1", "cz2", "cz3"], ["qc", "scc"])
     op("v", lambda: V.quantize_mx(T.qu[:, 0:128], T.su[:, 0:128], T.ut[:, 0:512]), ["ut"], ["qu", "su"])
     op("v", lambda: V.tensor_copy(T.qur[:, 0:128].bitcast(dt.uint32), T.qu[:, 0:128].bitcast(dt.uint32).indirect(T.upl[:, 0:8])),
        ["qu", "upl"], ["qur"])
@@ -186,12 +189,22 @@ def rank_program(g, core, T, topo):
             m = 16 * (a - 1)
             op("v", lambda: V.tensor_tensor(T.m16[:, 16 * a:16 * a + 16], T.mdg[:, m:m + 16], T.m16[:, 0:16], Op.add), ["mdg", "m160"], ["m16%d" % a])
 
-    def later2():
-        for a in (1, 2):
-            op("v", lambda: V.memset(T["et%d" % a][:, :], 0.0), [], ["et%d.%d" % (a, b) for b in range(4)])
-        op("v", lambda: V.tensor_scalar(T.ibe[:, :], T.ibd[:, :], 15, None, Op.bitwise_and), ["ibd"], ["ibe"])
-        op("v", lambda: V.tensor_scalar(T.dg2[:, :], T.ibe[:, :], 0.0, None, Op.is_equal), ["ibe"], ["dg2"])
+    def tiles():
+        op("v", lambda: V.quantize_mx(T.qc[:, 0:512], T.scc[:, 0:512], T.cz[:, 0:2048]), ["cz0", "cz1", "cz2", "cz3"], ["qc", "scc"])
+
+    def diagonal(a):
+        if a == 0:
+            op("v", lambda: V.tensor_scalar(T.ibe[:, :], T.ibd[:, :], 15, None, Op.bitwise_and), ["ibd"], ["ibe"])
+        else:
+            op("v", lambda: V.tensor_scalar(T.dg2[:, :], T.ibe[:, :], 0.0, None, Op.is_equal), ["ibe"], ["dg2"])
+
+    def last():
         op("v", lambda: V.quantize_mx(T.qv[:, 0:128], T.sv[:, 0:128], T.vt[:, 0:512]), ["vt"], ["qv", "sv"])
+    fill = [tiles, lambda: diagonal(1), last]
+
+    def zeros(a):
+        m = 2 * COUNT[a]
+        op("g", lambda: g.iota(T["et%d" % a][:, m:512], [[0, 512 - m]], 0, 0, allow_small_or_imprecise_dtypes=True), [], ["et%dz" % a])
 
     def slots(t):
         L, h, cn = LANES[t], LANES[t] // 2, T["cn%d" % t]
@@ -207,43 +220,60 @@ def rank_program(g, core, T, topo):
         qx, sx, xt = T["qx%d" % t], T["sx%d" % t], T["xt%d" % t]
         kq, ksx = "qx%d" % t, "sx%d" % t
         ct, lct, mx, bt = T["ct%d" % t], T["lct%d" % t], T["mx%d" % t], T["bt%d" % t]
-        kct, kbt = "ct%d" % t, "bt%d" % t
+        kct, kbt = ["ct%d%s" % (t, a) for a in ("a", "b", "c")], "bt%d" % t
         xk = ["xt0"] if t == 0 else ["xt%d.%d" % (t, b) for b in range(4)]
         op("v", lambda: V.quantize_mx(qx[:, 0:256], sx[:, 0:256], xt[:, 0:1024]), xk, [kq, ksx])
+        fill[t]()
         for a in range(2):
             op("p", lambda: P.matmul_mx(T.pg[:, 512 * a:512 * a + 128], T.qur[:, 0:128], T.sur[:, 0:128],
                                         qx[:, 128 * a:128 * a + 128], sx[:, 128 * a:128 * a + 128], True, True),
                ["qur", "sur", kq, ksx], ["pg%d" % a])
-        send(T["lqx%d" % t][:, 0:256].bitcast(dt.uint8), qx[:, 0:256].bitcast(dt.uint8), "ax%d" % t, [kq])
-        send(T["lsx%d" % t][:, 0:256], sx[:, 0:256], "ax%d" % t, [ksx])
+        send(T["lsx%d" % t][:, 0:256], sx[:, 0:256], "ax%d" % t, [ksx], scales_by)
+        send(T["lqx%d" % t][:, 0:256].bitcast(dt.uint8), qx[:, 0:256].bitcast(dt.uint8), "ax%d" % t, [kq], codes_by)
         if t == 0:
             slots(0)
-        op("v", lambda: V.tensor_copy(T.sco[:, 0:128], T.pg[:, 0:128]), ["pg0"], ["sco0"])
-        op("s", lambda: S.activation(T.sco[:, 128:256], T.pg[:, 512:640], COPY), ["pg1"], ["sco1"])
+        op("s", lambda: S.activation(T.sco[:, 0:128], T.pg[:, 0:128], COPY), ["pg0"], ["sco0"])
+        op("v", lambda: V.tensor_copy(T.sco[:, 128:256], T.pg[:, 512:640]), ["pg1"], ["sco1"])
         if t == 0:
-            lst, w, kl, lo, st, dg, kd = T.twt[:, 0:16], 256, "twt", 0, 1, T.dg1, "dg1"
+            lt, kl, w, w0, lo, st, dg, kd = T.twt, ["twt"], 256, 128, 0, 1, T.dg1, "dg1"
         else:
-            w, lo, st, dg, kd = COUNT[t - 1] + 16, 16, 2, T.dg2, "dg2"
-            lst, kl = T["ct%d" % (t - 1)][:, 0:w // 16], "ct%d" % (t - 1)
-        hi = lo + st * N
-        op("v", lambda: V.tensor_tensor(T.km[:, 0:w], T.sco[:, 0:256].indirect(lst), dg[:, 0:w], Op.mult), ["sco0", "sco1", kl, kd], ["km"])
-        op("s", lambda: S.activation(T.uu[:, 0:w], T.sco[:, 0:256].indirect(lst), COPY), ["sco0", "sco1", kl], ["uu"])
+            lt, kl, w, lo, st, dg, kd = T["ct%d" % (t - 1)], ["ct%d%s" % (t - 1, a) for a in ("a", "b", "c")], COUNT[t - 1] + 16, 16, 2, T.dg2, "dg2"
+            w0 = 16 * (C + 2 - C % 2)
+        for a, x, y in ((0, 0, w0), (1, w0, w)):
+            op("v", lambda: V.tensor_tensor(T.km[:, x:y], T.sco[:, 0:256].indirect(lt[:, x // 16:y // 16]), dg[:, x:y], Op.mult),
+               ["sco0", "sco1", kd] + kl, ["km%d" % a])
+        op("s", lambda: S.activation(T.uu[:, 0:w], T.sco[:, 0:256].indirect(lt[:, 0:w // 16]), COPY), ["sco0", "sco1"] + kl, ["uu"])
         if t == 0:
             op("s", lambda: S.activation(T.mx0[:, :], T.m16[:, 0:16].indirect(T.kapu[:, 0:16]), COPY), ["m160", "kapu"], ["mx0"])
             op("s", lambda: S.activation(T.bt0[:, :], T.win2[:, 0:256].indirect(T.twt[:, 0:16]), COPY), ["ramp", "twt"], ["bt0"])
-        op("v", lambda: V.tensor_tensor_scan(T.ks[:, 0:N], T.rs[:, 0:N], T.km[:, lo:hi:st], 0.0, Op.mult, Op.add), ["rs", "km"], ["ks"])
-        op("v", lambda: V.tensor_tensor(T.dd[:, 0:N], T.ks[:, 0:N].indirect(T.rept[:, 0:C]), T.uu[:, lo:hi:st], Op.subtract), ["ks", "rept", "uu"], ["dd"])
-        op("v", lambda: V.tensor_tensor(T.cmp[:, 0:N], T.dd[:, 0:N], mx[:, :], Op.is_lt), ["dd", "mx%d" % t], ["cmp"])
-        op("v", lambda: V.tensor_tensor_scan(T.pos[:, 0:N], T.rs[:, 0:N], T.cmp[:, 0:N], 0.0, Op.mult, Op.add), ["rs", "cmp"], ["pos"])
-        op("v", lambda: V.tensor_copy(T.post[:, 0:C], T.pos[:, 15:N:16]), ["pos"], ["post"])
-        op("v", lambda: V.tensor_tensor(T.sel[:, 0:N], T.win[:, 16 * t:16 * t + 16].indirect(T.post[:, 0:C]), bt[:, :], Op.mult), ["win", "post", kbt], ["sel"])
-        op("v", lambda: V.tensor_tensor_scan(T.ses[:, 0:N], T.rs[:, 0:N], T.sel[:, 0:N], 0.0, Op.mult, Op.add), ["rs", "sel"], ["ses"])
-        op("v", lambda: V.tensor_copy(ct[:, 1:C + 1], T.ses[:, 15:N:16]), ["ses"], [kct + "a"])
-        op("v", lambda: V.tensor_copy(ct[:, 0:1], T.ses[:, N - 1:N]), ["ses"], [kct])
-        send(lct[:, :], ct[:, :], "al%d" % t, [kct + "a", kct])
+        hc, N2 = C // 2, N // 2
+        halves = [(0, 0, hc, 0, N2), (1, hc, C, N2, N)]
+        for a, c0, c1, n0, n1 in halves:
+            op("v", lambda: V.tensor_tensor_scan(T.ks[:, n0:n1], T.rs[:, n0:n1], T.km[:, lo + st * n0:lo + st * n1:st], 0.0, Op.mult, Op.add),
+               ["rs", "km0", "km%d" % a], ["ks%d" % a])
+        for a, c0, c1, n0, n1 in halves:
+            op("v", lambda: V.tensor_tensor(T.dd[:, n0:n1], T.ks[:, n0:n1].indirect(T.rept[:, 0:hc]), T.uu[:, lo + st * n0:lo + st * n1:st], Op.subtract),
+               ["ks%d" % a, "rept", "uu"], ["dd%d" % a])
+        for a, c0, c1, n0, n1 in halves:
+            op("v", lambda: V.tensor_tensor(T.cmp[:, n0:n1], T.dd[:, n0:n1], mx[:, n0:n1], Op.is_lt), ["dd%d" % a, "mx%d" % t], ["cmp%d" % a])
+        for a, c0, c1, n0, n1 in halves:
+            op("v", lambda: V.tensor_tensor_scan(T.pos[:, n0:n1], T.rs[:, n0:n1], T.cmp[:, n0:n1], 0.0, Op.mult, Op.add), ["rs", "cmp%d" % a], ["pos%d" % a])
+        for a, c0, c1, n0, n1 in halves:
+            op("v", lambda: V.tensor_copy(T.post[:, c0:c1], T.pos[:, n0 + 15:n1:16]), ["pos%d" % a], ["post%d" % a])
+        for a, c0, c1, n0, n1 in halves:
+            op("v", lambda: V.tensor_tensor(T.sel[:, n0:n1], T.win[:, 16 * t:16 * t + 16].indirect(T.post[:, c0:c1]), bt[:, n0:n1], Op.mult),
+               ["win", "post%d" % a, kbt], ["sel%d" % a])
+        for a, c0, c1, n0, n1 in halves:
+            op("v", lambda: V.tensor_tensor_scan(T.ses[:, n0:n1], T.rs[:, n0:n1], T.sel[:, n0:n1], 0.0, Op.mult, Op.add), ["rs", "sel%d" % a], ["ses%d" % a])
+        op("v", lambda: V.tensor_copy(ct[:, 1:hc + 1], T.ses[:, 15:N2:16]), ["ses0"], [kct[0]])
+        op("v", lambda: V.tensor_copy(ct[:, hc + 1:C + 1], T.ses[:, N2 + 15:N:16]), ["ses1"], [kct[1]])
+        op("v", lambda: V.tensor_copy(ct[:, 0:1], T.ses[:, N - 1:N]), ["ses1"], [kct[2]])
+        send(lct[:, :], ct[:, :], "al%d" % t, kct, topo.engines(core, nxt))
         if t == 0:
             slots(1)
             slots(2)
+            zeros(1)
+            zeros(2)
 
         for b in range(4):
             op("p", lambda: P.matmul_mx(T.pf[:, 512 * b:512 * b + 256], T.qc[:, 128 * b:128 * b + 128], T.scc[:, 128 * b:128 * b + 128],
@@ -256,7 +286,7 @@ def rank_program(g, core, T, topo):
         if t == 0:
             later()
 
-        arrive("ax%d" % t, 2, ["lqx%d" % t])
+        arrive("ax%d" % t, n_state, ["lqx%d" % t])
 
         def arrived(b, q):
             dst, src = T.fp[:, 256 * b:256 * b + 256], T.pg[:, 512 * b:512 * b + 256]
@@ -265,16 +295,16 @@ def rank_program(g, core, T, topo):
             op("p", lambda: P.matmul_mx(T.pg[:, 512 * b:512 * b + 256], T.qc[:, 128 * b:128 * b + 128], T.scc[:, 128 * b:128 * b + 128],
                                         T["lqx%d" % t][:, 0:256], T["lsx%d" % t][:, 0:256], True, True), ["qc", "scc", "lqx%d" % t], ["pg%d" % b])
         on_s = [b for b in range(4) if b not in ONV[t]]
-        op("v", lambda: V.tensor_tensor(T.ef[:, 0:C], T.pos[:, 15:N:16], T.i16[:, 0:C], Op.add), ["pos", "i16"], ["ef"])
+        op("v", lambda: V.tensor_tensor(T.ef[:, 0:C], T.pos[:, 15:N:16], T.i16[:, 0:C], Op.add), ["pos0", "pos1", "i16"], ["ef"])
         if t < ROUNDS - 1:
             ctr, kr = T["ctr%d" % (t + 1)], "ctr%d" % (t + 1)
-            op("s", lambda: S.activation(ctr[:, :], T.win2[:, 0:256].indirect(ct[:, 0:C + 1]), COPY), ["ramp", kct + "a", kct], [kr])
+            op("s", lambda: S.activation(ctr[:, :], T.win2[:, 0:256].indirect(ct[:, 0:C + 1]), COPY), ["ramp"] + kct, [kr])
             op("s", lambda: S.activation(T.bta[:, 0:M], ctr[:, 16:16 + N:2], COPY, scale=T.loc[:, 0:1]), [kr, "loc"], ["bta"])
             op("s", lambda: S.activation(T.btb[:, 0:M], ctr[:, 17 - L:17 - L + N:2], COPY, scale=T.upc[:, 0:1]), [kr, "upc"], ["btb"])
         if t:
             arrived(on_s[0], "s")
             cb, brow = T["cb%d" % t], T["ctr%d" % t][:, 16:16 + 2 * N:2]
-            op("v", lambda: V.tensor_tensor(T.sel2[:, 0:N], T.win[:, 48:64].indirect(T.post[:, 0:C]), brow, Op.mult), ["win", "post", "ctr%d" % t], ["sel2"])
+            op("v", lambda: V.tensor_tensor(T.sel2[:, 0:N], T.win[:, 48:64].indirect(T.post[:, 0:C]), brow, Op.mult), ["win", "post0", "post1", "ctr%d" % t], ["sel2"])
             op("v", lambda: V.tensor_scalar(T.et[:, 0:C], T.ef[:, 0:C], float(16 - h), None, Op.add), ["ef"], ["et"])
             op("v", lambda: V.tensor_tensor_scan(T.ses2[:, 0:N], T.rs[:, 0:N], T.sel2[:, 0:N], 0.0, Op.mult, Op.add), ["rs", "sel2"], ["ses2"])
             op("v", lambda: V.tensor_copy(cb[:, 1:C + 1], T.ses2[:, 15:N:16]), ["ses2"], ["cba"])
@@ -295,30 +325,23 @@ def rank_program(g, core, T, topo):
         if t < ROUNDS - 1:
             op("v", lambda: V.tensor_tensor(T["bt%d" % (t + 1)][:, :], T.bta[:, 0:M], T.btb[:, 0:M], Op.add), ["bta", "btb"], ["bt%d" % (t + 1)])
         upt = T["upt%d" % (t + 1)]
-        if t == 0:
-            later2()
-        else:
-            for b in ONV[t]:
-                arrived(b, "v")
 
         def table():
-            if t == 0:
-                op("v", lambda: V.tensor_tensor(T.um[:, :], T.ur[:, :], T.dg1[:, :], Op.mult), ["ur", "dg1"], ["um"])
             op("v", lambda: V.tensor_tensor_scan(T.us[:, :], T.rs[:, :], T.um[:, :], 0.0, Op.mult, Op.add), ["rs", "um"], ["us"])
             op("v", lambda: V.tensor_copy(upt[:, :], T.us[:, 15:256:16]), ["us"], ["upt%d" % (t + 1)])
         if t == 0:
             op("v", lambda: V.tensor_copy(T.ur[:, 0:256].indirect(T.twt[:, 0:16]), T.win2[:, 256:512]), ["val", "twt"], ["ur"])
-            if not LATE[0]:
-                table()
+            op("v", lambda: V.tensor_tensor(T.um[:, :], T.ur[:, :], T.dg1[:, :], Op.mult), ["ur", "dg1"], ["um"])
+            table()
             for b in ONV[t]:
                 arrived(b, "v")
         else:
+            for b in ONV[t]:
+                arrived(b, "v")
             op("v", lambda: V.tensor_tensor(T.um[:, :], T.win2[:, 0:256 + N].indirect(T["upt%d" % t][:, 0:16]), T.dg1[:, :], Op.mult),
                ["ramp", "val", "upt%d" % t, "dg1"], ["um"])
-            if not LATE[t]:
-                table()
 
-        arrive("al%d" % t, 1, ["lct%d" % t])
+        arrive("al%d" % t, n_list, ["lct%d" % t])
         ee, ke = T["et%d" % t], "et%d" % t
         W = N + 16
 
@@ -341,11 +364,13 @@ def rank_program(g, core, T, topo):
         window(3)
         op("s", lambda: S.activation(T.f0[:, :], T.pf[:, 0:256], COPY), ["pf0"], ["f0"])
         qe, se, kqe = T["qe%d" % t], T["se%d" % t], "qe%d" % t
-        op("v", lambda: V.quantize_mx(qe[:, 0:128], se[:, 0:128], ee[:, 0:512]), [ke + ".%d" % b for b in range(4)], [kqe])
+        op("v", lambda: V.quantize_mx(qe[:, 0:128], se[:, 0:128], ee[:, 0:512]), [ke + ".%d" % b for b in range(4)] + ([ke + "z"] if t else []), [kqe])
         for b in (1, 0, 2, 3):
             op("p", lambda: P.matmul_mx(T.pg[:, 512 * b:512 * b + 128], T.wq[:, 128 * b:128 * b + 128], T.wsc[:, 128 * b:128 * b + 128],
                                         qe[:, 0:128], se[:, 0:128], True, True), ["wq", "wsc", kqe], ["pg%d" % b])
-        if LATE[t]:
+        if t == 0:
+            diagonal(0)
+        else:
             table()
         xn = T["xt%d" % (t + 1)]
         kup = "upt%d" % (t + 1)
@@ -373,7 +398,7 @@ def rank_program(g, core, T, topo):
         op("y", lambda: Y.dma_start(T.osc[4 * k:4 * k + 4, 0:256], T.sx3[32 * k:32 * k + 4, 0:256]), ["sx3"], [], "oa", 16)
     op("v", lambda: V.tensor_copy(T.ysb[:, 0:128], T.pg[:, 0:128]), ["pg0"], ["ya"])
     op("s", lambda: S.activation(T.ysb[:, 128:256], T.pg[:, 512:640], COPY), ["pg1"], ["yb"])
-    op("s", lambda: S.dma_start(T.y[:, 0:128], T.ysb[:, 0:128]), ["ya"], [], "ob", 16)
+    op("y", lambda: Y.dma_start(T.y[:, 0:128], T.ysb[:, 0:128]), ["ya"], [], "oa", 16)
     op("s", lambda: S.dma_start(T.y[:, 128:256], T.ysb[:, 128:256]), ["yb"], [], "ob", 16)
 
     for sem in count:

@@ -8,7 +8,6 @@ LANES = [16, 8, 4]
 COUNT = [16 * n for n in LANES]
 TINY = 1e-37
 HUGE = 1e28
-ONV = [[2, 3], [3], [3]]
 
 SCRATCH = {
     "ut": ("sbuf", [128, 512], "bfloat16"), "vt": ("sbuf", [128, 512], "bfloat16"), "twi": ("sbuf", [128, 16], "int32"),
@@ -19,12 +18,12 @@ SCRATCH = {
     "qv": ("sbuf", [128, 128], "float8_e4m3fn_x4"), "sv": ("sbuf", [128, 128], "uint8"),
     "cz": ("sbuf", [128, 2048], "bfloat16"), "half": ("sbuf", [128, 128], "bfloat16"), "idn": ("sbuf", [128, 128], "bfloat16"),
     "qc": ("sbuf", [128, 512], "float8_e4m3fn_x4"), "scc": ("sbuf", [128, 512], "uint8"),
-    "ib": ("sbuf", [128, 96], "int32"), "ibm": ("sbuf", [128, 96], "int32"),
-    "ibd": ("sbuf", [128, 272], "int32"), "ibe": ("sbuf", [128, 272], "int32"),
+    "ib": ("sbuf", [128, 96], "int32"), "ibm": ("sbuf", [128, 96], "int32"), "kf": ("sbuf", [128, 1], "float32"),
+    "dga": ("sbuf", [128, 17], "int32"), "dgb": ("sbuf", [128, 17], "int32"), "dgl": ("sbuf", [128, 17], "uint16"),
     "win": ("sbuf", [128, 64], "bfloat16"), "kapu": ("sbuf", [128, 16], "uint16"),
     "rept": ("sbuf", [128, 16], "uint16"), "upl": ("sbuf", [128, 8], "uint16"), "lnk": ("sbuf", [128, 17], "uint16"),
     "colv": ("sbuf", [128, 1], "float32"), "i16": ("sbuf", [128, 17], "float32"),
-    "r16": ("sbuf", [128, 256], "bfloat16"), "rs": ("sbuf", [128, 256], "bfloat16"),
+    "zz": ("sbuf", [128, 256], "bfloat16"), "rs": ("sbuf", [128, 256], "bfloat16"),
     "dg1": ("sbuf", [128, 256], "float32"), "dg2": ("sbuf", [128, 272], "float32"),
     "m16": ("sbuf", [128, 48], "float32"), "mc": ("sbuf", [128, 16], "float32"), "msh": ("sbuf", [128, 64], "int32"),
     "mdf": ("sbuf", [128, 32], "float32"), "mdg": ("sbuf", [128, 32], "float32"),
@@ -40,7 +39,8 @@ SCRATCH = {
     "us": ("sbuf", [128, 256], "float32"), "urow": ("sbuf", [128, 256], "float32"),
     "bta": ("sbuf", [128, 128], "bfloat16"), "btb": ("sbuf", [128, 128], "bfloat16"), "bt0": ("sbuf", [128, 256], "bfloat16"),
     "bt1": ("sbuf", [128, 128], "bfloat16"), "bt2": ("sbuf", [128, 64], "bfloat16"),
-    "fp": ("sbuf", [128, 1024], "bfloat16"), "fe": ("sbuf", [128, 4 * 272], "bfloat16"), "f0": ("sbuf", [128, 256], "bfloat16"),
+    "fp": ("sbuf", [128, 1024], "bfloat16"), "fe": ("sbuf", [128, 4 * 272], "bfloat16"),
+    "f0": ("sbuf", [128, 256], "bfloat16"), "f3": ("sbuf", [128, 128], "bfloat16"),
     "vw": ("sbuf", [128, 4 * 384], "bfloat16"), "nr": ("sbuf", [128, 1024], "bfloat16"), "ysb": ("sbuf", [128, 256], "float32"),
     "pf": ("psum", [128, 2048], "float32"), "pg": ("psum", [128, 2048], "float32"),
 }
@@ -144,63 +144,53 @@ def rank_program(g, core, T, topo):
     op("y", lambda: Y.dma_start(T.vt[:, :], T.v[:, :]), [], ["vt"], "lv", 16)
 
     op("v", lambda: V.memset(T.half[:, :], 0.5), [], ["half"])
+    op("v", lambda: V.memset(T.zz[:, :], 0.0), [], ["zz"])
     op("v", lambda: V.memset(T.cz[:, :], 0.0), [], ["cz"])
-    op("g", lambda: g.affine_select(T.idn[:, :], T.half[:, :], [[-1, 128]], Op.is_equal, 0.0, 0, 1), ["half"], ["idn"])
-    op("g", lambda: g.iota(T.i16[:, :], [[16, 17]], 0, 0, allow_small_or_imprecise_dtypes=True), [], ["i16"])
     for a, (pat, base, mul) in enumerate([([[16, 1], [1, 2], [2, 8]], 0, -1), ([[8, 2], [1, 2], [2, 4]], 0, -1),
                                           ([[4, 4], [1, 2], [2, 2]], 0, -1), ([[1, 16]], 0, -1),
                                           ([[0, 16]], 0, 1), ([[1, 16]], 0, 0)]):
         op("g", lambda: g.iota(T.ib[:, 16 * a:16 * a + 16], pat, base, mul), [], ["ib%d" % a])
-    op("g", lambda: g.iota(T.r16[:, :], [[0, 16], [1, 16]], 0, 0, allow_small_or_imprecise_dtypes=True), [], ["r16"])
+    op("g", lambda: g.iota(T.i16[:, :], [[16, 17]], 0, 0, allow_small_or_imprecise_dtypes=True), [], ["i16"])
+    op("g", lambda: g.affine_select(T.rs[:, :], T.zz[:, :], [[0, 16], [1, 16]], Op.is_equal, 1.0, 0, 0), ["zz"], ["rs"])
+    op("g", lambda: g.affine_select(T.idn[:, :], T.half[:, :], [[-1, 128]], Op.is_equal, 0.0, 0, 1), ["half"], ["idn"])
     op("g", lambda: g.iota(T.win2[:, 0:256], [[1, 256]], 0, 0, allow_small_or_imprecise_dtypes=True), [], ["ramp"])
-    op("g", lambda: g.iota(T.ibd[:, :], [[-1, 136], [0, 2]], 8, 1), [], ["ibd"])
 
-    for b in range(4):
-        op("s", lambda: S.activation(T.cz[:, 512 * b + b:512 * b + 512:4], T.idn[:, :], COPY), ["idn", "cz"], ["cz%d" % b])
-    op("v", lambda: V.tensor_scalar(T.upl[:, :], T.i16[:, 0:8], 1.0, None, Op.mult), ["i16"], ["upl"])
-    op("v", lambda: V.tensor_scalar(T.rept[:, :], T.i16[:, 0:16], 15.0, None, Op.add), ["i16"], ["rept"])
     op("v", lambda: V.tensor_scalar(T.ibm[:, :], T.ib[:, :], 15, None, Op.bitwise_and), ["ib%d" % a for a in range(6)], ["ibm"])
     op("v", lambda: V.tensor_scalar(T.win[:, :], T.ibm[:, 0:64], 0.0, None, Op.is_equal), ["ibm"], ["win"])
     op("v", lambda: V.tensor_copy(T.kapu[:, :], T.ibm[:, 64:80]), ["ibm"], ["kapu"])
-    op("v", lambda: V.tensor_tensor(T.mc[:, :], T.ibm[:, 80:96], T.ibm[:, 64:80], Op.is_lt), ["ibm"], ["mc"])
     op("s", lambda: S.activation(T.dg1[:, :], T.win[:, 48:64].indirect(T.kapu[:, 0:16]), COPY), ["win", "kapu"], ["dg1"])
+    op("v", lambda: V.tensor_copy(T.kf[:, :], T.ibm[:, 64:65]), ["ibm"], ["kf"])
+    op("v", lambda: V.tensor_tensor(T.mc[:, :], T.ibm[:, 80:96], T.ibm[:, 64:80], Op.is_lt), ["ibm"], ["mc"])
+    op("v", lambda: V.tensor_scalar(T.upl[:, :], T.i16[:, 0:8], 1.0, None, Op.mult), ["i16"], ["upl"])
+    op("v", lambda: V.tensor_scalar(T.dga[:, :], T.i16[:, :], T.kf[:, 0:1], 16.0, Op.add, Op.add), ["i16", "kf"], ["dga"])
     op("v", lambda: V.tensor_scalar(T.m16[:, 0:16], T.mc[:, :], TINY, None, Op.mult), ["mc"], ["m160"])
-    op("v", lambda: V.tensor_scalar(T.rs[:, :], T.r16[:, :], 1.0, None, Op.min), ["r16"], ["rs"])
+    op("v", lambda: V.tensor_scalar(T.colv[:, :], T.ibm[:, 64:65], 7.5, 2.0, Op.max, Op.mult), ["ibm"], ["colv"])
+    op("v", lambda: V.tensor_scalar(T.dgb[:, :], T.dga[:, :], 1, 15, Op.arith_shift_right, Op.bitwise_and), ["dga"], ["dgb"])
+    op("v", lambda: V.tensor_scalar(T.rept[:, :], T.i16[:, 0:16], 15.0, None, Op.add), ["i16"], ["rept"])
+    op("v", lambda: V.tensor_scalar(T.upi[:, :], T.ibm[:, 64:65], 1, None, Op.bitwise_and), ["ibm"], ["upi"])
+    op("v", lambda: V.tensor_copy(T.dgl[:, :], T.dgb[:, :]), ["dgb"], ["dgl"])
+    op("v", lambda: V.tensor_scalar(T.lnk[:, :], T.i16[:, :], T.colv[:, 0:1], 15.0, Op.add, Op.subtract), ["i16", "colv"], ["lnk"])
+    op("v", lambda: V.tensor_copy(T.upc[:, :], T.upi[:, :]), ["upi"], ["upc"])
+    op("v", lambda: V.tensor_scalar(T.loc[:, :], T.upi[:, :], -1.0, 1.0, Op.mult, Op.add), ["upi"], ["loc"])
+    for b in range(4):
+        op("s", lambda: S.activation(T.cz[:, 512 * b + b:512 * b + 512:4], T.idn[:, :], COPY), ["idn", "cz"], ["cz%d" % b])
     op("v", lambda: V.quantize_mx(T.qu[:, 0:128], T.su[:, 0:128], T.ut[:, 0:512]), ["ut"], ["qu", "su"])
     op("v", lambda: V.tensor_copy(T.qur[:, 0:128].bitcast(dt.uint32), T.qu[:, 0:128].bitcast(dt.uint32).indirect(T.upl[:, 0:8])),
        ["qu", "upl"], ["qur"])
     op("s", lambda: S.activation(T.sur[:, 0:128], T.su[:, 0:128].indirect(T.upl[:, 0:8]), COPY), ["su", "upl"], ["sur"])
     op("v", lambda: V.tensor_copy(T.twt[:, :], T.twi[:, :]), ["twi"], ["twt"])
 
-    def later():
+    def limits():
         for a in (1, 2):
             c = 32 * (a - 1)
             op("v", lambda: V.tensor_scalar(T.msh[:, c:c + 32], T.ibm[:, 64:96], 4 - a, None, Op.arith_shift_right), ["ibm"], ["msh%d" % a])
-        op("v", lambda: V.tensor_scalar(T.upi[:, :], T.ibm[:, 64:65], 1, None, Op.bitwise_and), ["ibm"], ["upi"])
-        op("v", lambda: V.tensor_scalar(T.colv[:, :], T.ibm[:, 64:65], 7.5, 2.0, Op.max, Op.mult), ["ibm"], ["colv"])
         for a in (1, 2):
             c, m = 32 * (a - 1), 16 * (a - 1)
             op("v", lambda: V.tensor_tensor(T.mdf[:, m:m + 16], T.msh[:, c:c + 16], T.msh[:, c + 16:c + 32], Op.subtract), ["msh%d" % a], ["mdf%d" % a])
-        op("v", lambda: V.tensor_copy(T.upc[:, :], T.upi[:, :]), ["upi"], ["upc"])
-        op("v", lambda: V.tensor_scalar(T.loc[:, :], T.upi[:, :], -1.0, 1.0, Op.mult, Op.add), ["upi"], ["loc"])
-        op("v", lambda: V.tensor_scalar(T.lnk[:, :], T.i16[:, :], T.colv[:, 0:1], 15.0, Op.add, Op.subtract), ["i16", "colv"], ["lnk"])
         op("v", lambda: V.tensor_scalar(T.mdg[:, :], T.mdf[:, :], HUGE, None, Op.mult), ["mdf1", "mdf2"], ["mdg"])
         for a in (1, 2):
             m = 16 * (a - 1)
             op("v", lambda: V.tensor_tensor(T.m16[:, 16 * a:16 * a + 16], T.mdg[:, m:m + 16], T.m16[:, 0:16], Op.add), ["mdg", "m160"], ["m16%d" % a])
-
-    def tiles():
-        op("v", lambda: V.quantize_mx(T.qc[:, 0:512], T.scc[:, 0:512], T.cz[:, 0:2048]), ["cz0", "cz1", "cz2", "cz3"], ["qc", "scc"])
-
-    def diagonal(a):
-        if a == 0:
-            op("v", lambda: V.tensor_scalar(T.ibe[:, :], T.ibd[:, :], 15, None, Op.bitwise_and), ["ibd"], ["ibe"])
-        else:
-            op("v", lambda: V.tensor_scalar(T.dg2[:, :], T.ibe[:, :], 0.0, None, Op.is_equal), ["ibe"], ["dg2"])
-
-    def last():
-        op("v", lambda: V.quantize_mx(T.qv[:, 0:128], T.sv[:, 0:128], T.vt[:, 0:512]), ["vt"], ["qv", "sv"])
-    fill = [tiles, lambda: diagonal(1), last]
 
     def zeros(a):
         m = 2 * COUNT[a]
@@ -221,16 +211,27 @@ def rank_program(g, core, T, topo):
         kq, ksx = "qx%d" % t, "sx%d" % t
         ct, lct, mx, bt = T["ct%d" % t], T["lct%d" % t], T["mx%d" % t], T["bt%d" % t]
         kct, kbt = ["ct%d%s" % (t, a) for a in ("a", "b", "c")], "bt%d" % t
-        xk = ["xt0"] if t == 0 else ["xt%d.%d" % (t, b) for b in range(4)]
+        xk = ["xt0"] if t == 0 else ["xt%d.%s" % (t, b) for b in ("f0", "f3", 1, 2, 3)]
         op("v", lambda: V.quantize_mx(qx[:, 0:256], sx[:, 0:256], xt[:, 0:1024]), xk, [kq, ksx])
-        fill[t]()
+        if t == 0:
+            op("v", lambda: V.quantize_mx(T.qc[:, 0:512], T.scc[:, 0:512], T.cz[:, 0:2048]), ["cz0", "cz1", "cz2", "cz3"], ["qc", "scc"])
+        else:
+            op("v", lambda: V.tensor_tensor(bt[:, :], T.bta[:, 0:N], T.btb[:, 0:N], Op.add), ["bta", "btb"], [kbt])
+        if t == 1:
+            op("v", lambda: V.quantize_mx(T.qv[:, 0:128], T.sv[:, 0:128], T.vt[:, 0:512]), ["vt"], ["qv", "sv"])
         for a in range(2):
             op("p", lambda: P.matmul_mx(T.pg[:, 512 * a:512 * a + 128], T.qur[:, 0:128], T.sur[:, 0:128],
                                         qx[:, 128 * a:128 * a + 128], sx[:, 128 * a:128 * a + 128], True, True),
                ["qur", "sur", kq, ksx], ["pg%d" % a])
-        send(T["lsx%d" % t][:, 0:256], sx[:, 0:256], "ax%d" % t, [ksx], scales_by)
-        send(T["lqx%d" % t][:, 0:256].bitcast(dt.uint8), qx[:, 0:256].bitcast(dt.uint8), "ax%d" % t, [kq], codes_by)
+
+        def scales():
+            send(T["lsx%d" % t][:, 0:256], sx[:, 0:256], "ax%d" % t, [ksx], scales_by)
         if t == 0:
+            scales()
+        send(T["lqx%d" % t][:, 0:256].bitcast(dt.uint8), qx[:, 0:256].bitcast(dt.uint8), "ax%d" % t, [kq], codes_by)
+        if t:
+            scales()
+        else:
             slots(0)
         op("s", lambda: S.activation(T.sco[:, 0:128], T.pg[:, 0:128], COPY), ["pg0"], ["sco0"])
         op("v", lambda: V.tensor_copy(T.sco[:, 128:256], T.pg[:, 512:640]), ["pg1"], ["sco1"])
@@ -284,7 +285,7 @@ def rank_program(g, core, T, topo):
         for b in (0, 1, 2):
             window(b)
         if t == 0:
-            later()
+            op("s", lambda: S.activation(T.dg2[:, :], T.win[:, 48:64].indirect(T.dgl[:, 0:17]), COPY), ["win", "dgl"], ["dg2"])
 
         arrive("ax%d" % t, n_state, ["lqx%d" % t])
 
@@ -294,15 +295,32 @@ def rank_program(g, core, T, topo):
         for b in range(4):
             op("p", lambda: P.matmul_mx(T.pg[:, 512 * b:512 * b + 256], T.qc[:, 128 * b:128 * b + 128], T.scc[:, 128 * b:128 * b + 128],
                                         T["lqx%d" % t][:, 0:256], T["lsx%d" % t][:, 0:256], True, True), ["qc", "scc", "lqx%d" % t], ["pg%d" % b])
-        on_s = [b for b in range(4) if b not in ONV[t]]
+
+        def renewed():
+            op("s", lambda: S.activation(T.win2[:, 256:256 + N], T.vwx[:, 0:N + 16].indirect(T.et[:, 0:C]), COPY), ["vwx", "et"], ["val"])
         op("v", lambda: V.tensor_tensor(T.ef[:, 0:C], T.pos[:, 15:N:16], T.i16[:, 0:C], Op.add), ["pos0", "pos1", "i16"], ["ef"])
         if t < ROUNDS - 1:
             ctr, kr = T["ctr%d" % (t + 1)], "ctr%d" % (t + 1)
             op("s", lambda: S.activation(ctr[:, :], T.win2[:, 0:256].indirect(ct[:, 0:C + 1]), COPY), ["ramp"] + kct, [kr])
             op("s", lambda: S.activation(T.bta[:, 0:M], ctr[:, 16:16 + N:2], COPY, scale=T.loc[:, 0:1]), [kr, "loc"], ["bta"])
             op("s", lambda: S.activation(T.btb[:, 0:M], ctr[:, 17 - L:17 - L + N:2], COPY, scale=T.upc[:, 0:1]), [kr, "upc"], ["btb"])
-        if t:
-            arrived(on_s[0], "s")
+        upt = T["upt%d" % (t + 1)]
+        if t == 0:
+            op("v", lambda: V.tensor_scalar(T.et[:, 0:C], T.ef[:, 0:C], float(16 - h), None, Op.add), ["ef"], ["et"])
+            op("v", lambda: V.tensor_tensor(T.vwx[:, 0:N + 16], ctr[:, :].indirect(T.lnk[:, 0:C + 1]), T.cn0[:, :], Op.max), [kr, "lnk", "cn0"], ["vwx"])
+            renewed()
+            limits()
+            for a in (1, 2):
+                op("s", lambda: S.activation(T["mx%d" % a][:, :], T.m16[:, 16 * a:16 * a + 16].indirect(T.kapu[:, 0:COUNT[a] // 16]), COPY),
+                   ["m16%d" % a, "kapu"], ["mx%d" % a])
+            for b in (0, 1, 2):
+                arrived(b, "s")
+            op("v", lambda: V.tensor_copy(T.ur[:, 0:256].indirect(T.twt[:, 0:16]), T.win2[:, 256:512]), ["val", "twt"], ["ur"])
+            op("v", lambda: V.tensor_tensor(T.um[:, :], T.ur[:, :], T.dg1[:, :], Op.mult), ["ur", "dg1"], ["um"])
+            arrived(3, "v")
+        else:
+            for b in (0, 1, 2):
+                arrived(b, "s")
             cb, brow = T["cb%d" % t], T["ctr%d" % t][:, 16:16 + 2 * N:2]
             op("v", lambda: V.tensor_tensor(T.sel2[:, 0:N], T.win[:, 48:64].indirect(T.post[:, 0:C]), brow, Op.mult), ["win", "post0", "post1", "ctr%d" % t], ["sel2"])
             op("v", lambda: V.tensor_scalar(T.et[:, 0:C], T.ef[:, 0:C], float(16 - h), None, Op.add), ["ef"], ["et"])
@@ -311,33 +329,8 @@ def rank_program(g, core, T, topo):
             op("v", lambda: V.tensor_copy(cb[:, 0:1], T.ses2[:, N - 1:N]), ["ses2"], ["cb"])
             op("v", lambda: V.tensor_tensor(T.vwx[:, 0:N + 16], T.win2[:, 0:256].indirect(cb[:, 0:C + 1]), T["cn%d" % t][:, :], Op.max),
                ["ramp", "cba", "cb", "cn%d" % t], ["vwx"])
-        else:
-            op("v", lambda: V.tensor_scalar(T.et[:, 0:C], T.ef[:, 0:C], float(16 - h), None, Op.add), ["ef"], ["et"])
-            op("v", lambda: V.tensor_tensor(T.vwx[:, 0:N + 16], ctr[:, :].indirect(T.lnk[:, 0:C + 1]), T.cn0[:, :], Op.max), [kr, "lnk", "cn0"], ["vwx"])
-        op("s", lambda: S.activation(T.win2[:, 256:256 + N], T.vwx[:, 0:N + 16].indirect(T.et[:, 0:C]), COPY), ["vwx", "et"], ["val"])
-        if t == 0:
-            for a in (1, 2):
-                op("s", lambda: S.activation(T["mx%d" % a][:, :], T.m16[:, 16 * a:16 * a + 16].indirect(T.kapu[:, 0:COUNT[a] // 16]), COPY),
-                   ["m16%d" % a, "kapu"], ["mx%d" % a])
-            arrived(on_s[0], "s")
-        for b in on_s[1:]:
-            arrived(b, "s")
-        if t < ROUNDS - 1:
-            op("v", lambda: V.tensor_tensor(T["bt%d" % (t + 1)][:, :], T.bta[:, 0:M], T.btb[:, 0:M], Op.add), ["bta", "btb"], ["bt%d" % (t + 1)])
-        upt = T["upt%d" % (t + 1)]
-
-        def table():
-            op("v", lambda: V.tensor_tensor_scan(T.us[:, :], T.rs[:, :], T.um[:, :], 0.0, Op.mult, Op.add), ["rs", "um"], ["us"])
-            op("v", lambda: V.tensor_copy(upt[:, :], T.us[:, 15:256:16]), ["us"], ["upt%d" % (t + 1)])
-        if t == 0:
-            op("v", lambda: V.tensor_copy(T.ur[:, 0:256].indirect(T.twt[:, 0:16]), T.win2[:, 256:512]), ["val", "twt"], ["ur"])
-            op("v", lambda: V.tensor_tensor(T.um[:, :], T.ur[:, :], T.dg1[:, :], Op.mult), ["ur", "dg1"], ["um"])
-            table()
-            for b in ONV[t]:
-                arrived(b, "v")
-        else:
-            for b in ONV[t]:
-                arrived(b, "v")
+            renewed()
+            arrived(3, "v")
             op("v", lambda: V.tensor_tensor(T.um[:, :], T.win2[:, 0:256 + N].indirect(T["upt%d" % t][:, 0:16]), T.dg1[:, :], Op.mult),
                ["ramp", "val", "upt%d" % t, "dg1"], ["um"])
 
@@ -353,40 +346,49 @@ def rank_program(g, core, T, topo):
         def mean(b):
             op("v", lambda: V.tensor_tensor(ee[:, b:4 * M:4], T.fe[:, 272 * b + 16:272 * b + 16 + N:2],
                                             T.fe[:, 272 * b + 17 - L:272 * b + 17 - L + N:2], Op.add), ["fe%d" % b], [ke + ".%d" % b])
-        own_b = ONV[t][-1]
-        order = [b for b in range(4) if b != own_b]
-        ends("v", own_b)
-        for b in order:
+        ends("v", 3)
+        for b in (0, 1, 2):
             ends("s", b)
-        mean(own_b)
-        for b in order:
+        for b in (3, 0, 1, 2):
             mean(b)
         window(3)
         op("s", lambda: S.activation(T.f0[:, :], T.pf[:, 0:256], COPY), ["pf0"], ["f0"])
+        op("s", lambda: S.activation(T.f3[:, :], T.pf[:, 1664:1792], COPY), ["pf3"], ["f3"])
         qe, se, kqe = T["qe%d" % t], T["se%d" % t], "qe%d" % t
         op("v", lambda: V.quantize_mx(qe[:, 0:128], se[:, 0:128], ee[:, 0:512]), [ke + ".%d" % b for b in range(4)] + ([ke + "z"] if t else []), [kqe])
         for b in (1, 0, 2, 3):
             op("p", lambda: P.matmul_mx(T.pg[:, 512 * b:512 * b + 128], T.wq[:, 128 * b:128 * b + 128], T.wsc[:, 128 * b:128 * b + 128],
                                         qe[:, 0:128], se[:, 0:128], True, True), ["wq", "wsc", kqe], ["pg%d" % b])
-        if t == 0:
-            diagonal(0)
-        else:
-            table()
+        op("v", lambda: V.tensor_tensor_scan(T.us[:, :], T.rs[:, :], T.um[:, :], 0.0, Op.mult, Op.add), ["rs", "um"], ["us"])
+        op("v", lambda: V.tensor_copy(upt[:, :], T.us[:, 15:256:16]), ["us"], ["upt%d" % (t + 1)])
         xn = T["xt%d" % (t + 1)]
         kup = "upt%d" % (t + 1)
-        for b in (1, 0, 2, 3):
-            op("v", lambda: V.tensor_scalar(T.vw[:, 384 * b + 256:384 * b + 256 + M], T.pg[:, 512 * b:512 * b + M], 0.015625, None, Op.mult),
+
+        def made(q, b):
+            dst, src = T.vw[:, 384 * b + 256:384 * b + 256 + M], T.pg[:, 512 * b:512 * b + M]
+            op(q, lambda: V.tensor_scalar(dst, src, 0.015625, None, Op.mult) if q == "v" else S.activation(dst, src, COPY, scale=0.015625),
                ["pg%d" % b], ["vwh%d" % b])
-        for b in (1, 2, 3):
-            op("s", lambda: S.activation(T.nr[:, 256 * b:256 * b + 256], T.vw[:, 384 * b:384 * b + 256 + M].indirect(upt[:, 0:16]), COPY),
+        made("s", 1)
+        for b in (0, 2, 3):
+            made("v", b)
+        for b, n in ((1, 256), (2, 256), (3, 128)):
+            op("s", lambda: S.activation(T.nr[:, 256 * b:256 * b + n], T.vw[:, 384 * b:384 * b + 256 + M].indirect(upt[:, 0:n // 16]), COPY),
                ["vwf%d" % b, "vwh%d" % b, kup], ["nr%d" % b])
-        op("v", lambda: V.tensor_tensor(xn[:, 0:1024:4], T.vw[:, 0:256 + M].indirect(upt[:, 0:16]), T.f0[:, :], Op.add),
-           ["vwf0", "vwh0", "f0", kup], ["xt%d.0" % (t + 1)])
-        for b in (1, 2, 3):
-            op("v", lambda: V.tensor_tensor(xn[:, b:1024:4], T.pf[:, 512 * b:512 * b + 256], T.nr[:, 256 * b:256 * b + 256], Op.add),
+
+        def both(b, x, f, k):
+            op("v", lambda: V.tensor_tensor(xn[:, 4 * x + b:1024:4], T.vw[:, 384 * b:384 * b + 256 + M].indirect(upt[:, x // 16:16]), f[:, :], Op.add),
+               ["vwf%d" % b, "vwh%d" % b, k, kup], ["xt%d.%s" % (t + 1, k)])
+
+        def blend(b, n):
+            op("v", lambda: V.tensor_tensor(xn[:, b:4 * n:4], T.pf[:, 512 * b:512 * b + n], T.nr[:, 256 * b:256 * b + n], Op.add),
                ["pf%d" % b, "nr%d" % b], ["xt%d.%d" % (t + 1, b)])
+        both(0, 0, T.f0, "f0")
+        blend(1, 256)
+        both(3, 128, T.f3, "f3")
+        blend(2, 256)
+        blend(3, 128)
         if t == ROUNDS - 1:
-            op("v", lambda: V.quantize_mx(T.qx3[:, 0:256], T.sx3[:, 0:256], xn[:, 0:1024]), ["xt3.%d" % b for b in range(4)], ["qx3", "sx3"])
+            op("v", lambda: V.quantize_mx(T.qx3[:, 0:256], T.sx3[:, 0:256], xn[:, 0:1024]), ["xt3.%s" % b for b in ("f0", "f3", 1, 2, 3)], ["qx3", "sx3"])
             op("s", lambda: S.activation(T.urow[:, :], T.win2[:, 0:256 + N].indirect(T["upt%d" % t][:, 0:16]), COPY), ["ramp", "val", "upt%d" % t], ["urow"])
             op("y", lambda: Y.dma_start(T.op[:, :], T.urow[0:128:16, :]), ["urow"], [], "oo", 16)
 

import numpy as np
from concourse.mybir import dt, AluOpType, ActivationFunctionType

Op = AluOpType
COPY = ActivationFunctionType.Copy
ROUNDS, PLACES = 3, 256
LANES = [16, 8, 4]
COUNT = [16 * n for n in LANES]
TINY = 1e-37
HUGE = 1e28

SCRATCH = {
    "ut": ("sbuf", [128, 512], "bfloat16"), "vt": ("sbuf", [128, 512], "bfloat16"), "twi": ("sbuf", [128, 16], "int32"),
    "twt": ("sbuf", [128, 16], "uint16"),
    "wq": ("sbuf", [128, 512], "float8_e4m3fn_x4"), "wsc": ("sbuf", [128, 512], "uint8"),
    "qu": ("sbuf", [128, 128], "float8_e4m3fn_x4"), "su": ("sbuf", [128, 128], "uint8"),
    "qur": ("sbuf", [128, 128], "float8_e4m3fn_x4"), "sur": ("sbuf", [128, 128], "uint8"),
    "qv": ("sbuf", [128, 128], "float8_e4m3fn_x4"), "sv": ("sbuf", [128, 128], "uint8"),
    "cz": ("sbuf", [128, 2048], "bfloat16"), "half": ("sbuf", [128, 128], "bfloat16"), "idn": ("sbuf", [128, 128], "bfloat16"),
    "qc": ("sbuf", [128, 512], "float8_e4m3fn_x4"), "scc": ("sbuf", [128, 512], "uint8"),
    "ib": ("sbuf", [128, 96], "int32"), "ibm": ("sbuf", [128, 96], "int32"), "kf": ("sbuf", [128, 1], "float32"),
    "dga": ("sbuf", [128, 17], "int32"), "dgb": ("sbuf", [128, 17], "int32"), "dgl": ("sbuf", [128, 17], "uint16"),
    "win": ("sbuf", [128, 64], "bfloat16"), "kapu": ("sbuf", [128, 16], "uint16"),
    "rept": ("sbuf", [128, 16], "uint16"), "upl": ("sbuf", [128, 8], "uint16"), "lnk": ("sbuf", [128, 17], "uint16"),
    "colv": ("sbuf", [128, 1], "float32"), "i16": ("sbuf", [128, 17], "float32"),
    "zz": ("sbuf", [128, 256], "bfloat16"), "rs": ("sbuf", [128, 256], "bfloat16"),
    "dg1": ("sbuf", [128, 256], "float32"), "dg2": ("sbuf", [128, 272], "float32"),
    "m16": ("sbuf", [128, 48], "float32"), "mc": ("sbuf", [128, 16], "float32"), "msh": ("sbuf", [128, 64], "int32"),
    "mdf": ("sbuf", [128, 32], "float32"), "mdg": ("sbuf", [128, 32], "float32"),
    "upi": ("sbuf", [128, 1], "int32"), "upc": ("sbuf", [128, 1], "float32"), "loc": ("sbuf", [128, 1], "float32"),
    "win2": ("sbuf", [128, 512], "float32"),
    "sco": ("sbuf", [128, 256], "float32"), "km": ("sbuf", [128, 272], "float32"), "uu": ("sbuf", [128, 272], "float32"),
    "ks": ("sbuf", [128, 256], "float32"), "dd": ("sbuf", [128, 256], "float32"),
    "cmp": ("sbuf", [128, 256], "bfloat16"), "pos": ("sbuf", [128, 256], "bfloat16"),
    "sel": ("sbuf", [128, 256], "bfloat16"), "ses": ("sbuf", [128, 256], "bfloat16"),
    "sel2": ("sbuf", [128, 128], "bfloat16"), "ses2": ("sbuf", [128, 128], "bfloat16"),
    "ef": ("sbuf", [128, 16], "float32"), "et": ("sbuf", [128, 16], "uint16"), "post": ("sbuf", [128, 16], "uint16"),
    "vwx": ("sbuf", [128, 272], "float32"), "ur": ("sbuf", [128, 256], "float32"), "um": ("sbuf", [128, 256], "float32"),
    "us": ("sbuf", [128, 256], "float32"), "urow": ("sbuf", [128, 256], "float32"),
    "bta": ("sbuf", [128, 128], "bfloat16"), "btb": ("sbuf", [128, 128], "bfloat16"), "bt0": ("sbuf", [128, 256], "bfloat16"),
    "bt1": ("sbuf", [128, 128], "bfloat16"), "bt2": ("sbuf", [128, 64], "bfloat16"),
    "fp": ("sbuf", [128, 1024], "bfloat16"), "fe": ("sbuf", [128, 4 * 272], "bfloat16"),
    "f0": ("sbuf", [128, 256], "bfloat16"), "f3": ("sbuf", [128, 128], "bfloat16"),
    "vw": ("sbuf", [128, 4 * 384], "bfloat16"), "nr": ("sbuf", [128, 1024], "bfloat16"), "ysb": ("sbuf", [128, 256], "float32"),
    "pf": ("psum", [128, 2048], "float32"), "pg": ("psum", [128, 2048], "float32"),
}
for _t in range(4):
    SCRATCH["xt%d" % _t] = ("sbuf", [128, 1024], "bfloat16")
    SCRATCH["qx%d" % _t] = ("sbuf", [128, 256], "float8_e4m3fn_x4")
    SCRATCH["sx%d" % _t] = ("sbuf", [128, 256], "uint8")
    if _t:
        SCRATCH["upt%d" % _t] = ("sbuf", [128, 16], "uint16")
for _t in range(3):
    _c = COUNT[_t] // 16
    SCRATCH["lqx%d" % _t] = ("sbuf", [128, 256], "float8_e4m3fn_x4")
    SCRATCH["lsx%d" % _t] = ("sbuf", [128, 256], "uint8")
    SCRATCH["ct%d" % _t] = ("sbuf", [128, _c + 1], "uint16")
    SCRATCH["lct%d" % _t] = ("sbuf", [128, _c + 1], "uint16")
    SCRATCH["cn%d" % _t] = ("sbuf", [128, COUNT[_t] + 16], "float32")
    SCRATCH["mx%d" % _t] = ("sbuf", [128, COUNT[_t]], "float32")
    SCRATCH["et%d" % _t] = ("sbuf", [128, 512], "bfloat16")
    SCRATCH["qe%d" % _t] = ("sbuf", [128, 128], "float8_e4m3fn_x4")
    SCRATCH["se%d" % _t] = ("sbuf", [128, 128], "uint8")
    if _t:
        SCRATCH["ctr%d" % _t] = ("sbuf", [128, COUNT[_t - 1] + 16], "bfloat16")
        SCRATCH["cb%d" % _t] = ("sbuf", [128, _c + 1], "uint16")

SEMAPHORES = (["v", "s", "p", "gq", "lx", "lu", "lt", "lw", "lws", "lv", "snt", "oa", "ob", "oo"]
              + ["ax%d" % t for t in range(3)] + ["al%d" % t for t in range(3)])


def rank_program(g, core, T, topo):
    rank = T.rank_of(core)
    if rank is None:
        return
    cores = T.cores
    nxt, prv = cores[(rank + 1) % len(cores)], cores[(rank - 1) % len(cores)]

    def shares(a, b):
        e = topo.engines(a, b)
        return (e[:8], e[8:]) if len(e) > 8 else (e, e)
    codes_by, scales_by = shares(core, nxt)
    n_list, n_state = len(topo.engines(prv, core)), sum(len(e) for e in shares(prv, core))
    rid, pid = topo.addr(nxt)[0], topo.addr(nxt)[1]

    eng = {"g": g, "v": g.vector, "s": g.scalar, "p": g.tensor, "y": g.sync}
    own = {"g": "gq", "v": "v", "s": "s", "p": "p"}
    count, waited = {}, {}
    known = {q: {} for q in eng}
    writer, readers = {}, {}

    def need(q, toks):
        for sem, val, clock in sorted(toks, key=lambda k: -len(k[2])):
            if known[q].get(sem, 0) >= val:
                continue
            best = max(v for s, v, c in toks if s == sem)
            eng[q].wait_ge(T.sem[sem], best)
            waited[sem] = max(waited.get(sem, 0), best)
            for s, v, c in toks:
                if s == sem:
                    for a in c:
                        known[q][a] = max(known[q].get(a, 0), c[a])
            known[q][sem] = max(known[q].get(sem, 0), best)

    def deps(q, reads, writes):
        toks = [writer[k] for k in reads if k in writer]
        for k in writes:
            if k in writer:
                toks.append(writer[k])
            toks += readers.get(k, [])
        need(q, toks)

    def op(q, call, reads, writes, sem=None, inc=1):
        deps(q, reads, writes)
        sem = sem or own[q]
        count[sem] = count.get(sem, 0) + inc
        call().then_inc(T.sem[sem], inc)
        tok = (sem, count[sem], dict(known[q]))
        for k in reads:
            readers.setdefault(k, []).append(tok)
        for k in writes:
            writer[k] = tok
            readers[k] = []

    V, S, P, Y = g.vector, g.scalar, g.tensor, g.sync

    def send(out_ap, in_ap, sem, reads, by):
        deps("g", reads, [])
        g.remote_dma(out_ap=out_ap, in_ap=in_ap, remote_sem=T.sem[sem], local_sem=T.sem.snt, pid=pid, routing_id=rid,
                     dma_engine_mask=sum(1 << e for e in by))
        count["snt"] = count.get("snt", 0) + len(by)

    def arrive(sem, n, keys):
        count[sem] = n
        for k in keys:
            writer[k] = (sem, n, {})

    op("y", lambda: Y.dma_start(T.xt0[:, :], T.x[:, :]), [], ["xt0"], "lx", 16)
    op("s", lambda: S.dma_start(T.ut[:, :], T.u[:, :]), [], ["ut"], "lu", 16)
    op("s", lambda: S.dma_start(T.twi[:, :], T.tw[:, :]), [], ["twi"], "lt", 16)
    deps("y", ["xt0"], [])
    op("y", lambda: Y.dma_start(T.wq[:, 0:512].bitcast(dt.uint8), T.wc[:, 0:2048]), [], ["wq"], "lw", 16)
    op("y", lambda: Y.dma_start(T.wsc[:, 0:512], T.ws[:, 0:512]), [], ["wsc"], "lws", 16)
    op("y", lambda: Y.dma_start(T.vt[:, :], T.v[:, :]), [], ["vt"], "lv", 16)

    op("v", lambda: V.memset(T.half[:, :], 0.5), [], ["half"])
    op("v", lambda: V.memset(T.zz[:, :], 0.0), [], ["zz"])
    op("v", lambda: V.memset(T.cz[:, :], 0.0), [], ["cz"])
    for a, (pat, base, mul) in enumerate([([[16, 1], [1, 2], [2, 8]], 0, -1), ([[8, 2], [1, 2], [2, 4]], 0, -1),
                                          ([[4, 4], [1, 2], [2, 2]], 0, -1), ([[1, 16]], 0, -1),
                                          ([[0, 16]], 0, 1), ([[1, 16]], 0, 0)]):
        op("g", lambda: g.iota(T.ib[:, 16 * a:16 * a + 16], pat, base, mul), [], ["ib%d" % a])
    op("g", lambda: g.iota(T.i16[:, :], [[16, 17]], 0, 0, allow_small_or_imprecise_dtypes=True), [], ["i16"])
    op("g", lambda: g.affine_select(T.rs[:, :], T.zz[:, :], [[0, 16], [1, 16]], Op.is_equal, 1.0, 0, 0), ["zz"], ["rs"])
    op("g", lambda: g.affine_select(T.idn[:, :], T.half[:, :], [[-1, 128]], Op.is_equal, 0.0, 0, 1), ["half"], ["idn"])
    op("g", lambda: g.iota(T.win2[:, 0:256], [[1, 256]], 0, 0, allow_small_or_imprecise_dtypes=True), [], ["ramp"])

    op("v", lambda: V.tensor_scalar(T.ibm[:, :], T.ib[:, :], 15, None, Op.bitwise_and), ["ib%d" % a for a in range(6)], ["ibm"])
    op("v", lambda: V.tensor_scalar(T.win[:, :], T.ibm[:, 0:64], 0.0, None, Op.is_equal), ["ibm"], ["win"])
    op("v", lambda: V.tensor_copy(T.kapu[:, :], T.ibm[:, 64:80]), ["ibm"], ["kapu"])
    op("s", lambda: S.activation(T.dg1[:, :], T.win[:, 48:64].indirect(T.kapu[:, 0:16]), COPY), ["win", "kapu"], ["dg1"])
    op("v", lambda: V.tensor_copy(T.kf[:, :], T.ibm[:, 64:65]), ["ibm"], ["kf"])
    op("v", lambda: V.tensor_tensor(T.mc[:, :], T.ibm[:, 80:96], T.ibm[:, 64:80], Op.is_lt), ["ibm"], ["mc"])
    op("v", lambda: V.tensor_scalar(T.upl[:, :], T.i16[:, 0:8], 1.0, None, Op.mult), ["i16"], ["upl"])
    op("v", lambda: V.tensor_scalar(T.dga[:, :], T.i16[:, :], T.kf[:, 0:1], 16.0, Op.add, Op.add), ["i16", "kf"], ["dga"])
    op("v", lambda: V.tensor_scalar(T.m16[:, 0:16], T.mc[:, :], TINY, None, Op.mult), ["mc"], ["m160"])
    op("v", lambda: V.tensor_scalar(T.colv[:, :], T.ibm[:, 64:65], 7.5, 2.0, Op.max, Op.mult), ["ibm"], ["colv"])
    op("v", lambda: V.tensor_scalar(T.dgb[:, :], T.dga[:, :], 1, 15, Op.arith_shift_right, Op.bitwise_and), ["dga"], ["dgb"])
    op("v", lambda: V.tensor_scalar(T.rept[:, :], T.i16[:, 0:16], 15.0, None, Op.add), ["i16"], ["rept"])
    op("v", lambda: V.tensor_scalar(T.upi[:, :], T.ibm[:, 64:65], 1, None, Op.bitwise_and), ["ibm"], ["upi"])
    op("v", lambda: V.tensor_copy(T.dgl[:, :], T.dgb[:, :]), ["dgb"], ["dgl"])
    op("v", lambda: V.tensor_scalar(T.lnk[:, :], T.i16[:, :], T.colv[:, 0:1], 15.0, Op.add, Op.subtract), ["i16", "colv"], ["lnk"])
    op("v", lambda: V.tensor_copy(T.upc[:, :], T.upi[:, :]), ["upi"], ["upc"])
    op("v", lambda: V.tensor_scalar(T.loc[:, :], T.upi[:, :], -1.0, 1.0, Op.mult, Op.add), ["upi"], ["loc"])
    for b in range(4):
        op("s", lambda: S.activation(T.cz[:, 512 * b + b:512 * b + 512:4], T.idn[:, :], COPY), ["idn", "cz"], ["cz%d" % b])
    op("v", lambda: V.quantize_mx(T.qu[:, 0:128], T.su[:, 0:128], T.ut[:, 0:512]), ["ut"], ["qu", "su"])
    op("v", lambda: V.tensor_copy(T.qur[:, 0:128].bitcast(dt.uint32), T.qu[:, 0:128].bitcast(dt.uint32).indirect(T.upl[:, 0:8])),
       ["qu", "upl"], ["qur"])
    op("s", lambda: S.activation(T.sur[:, 0:128], T.su[:, 0:128].indirect(T.upl[:, 0:8]), COPY), ["su", "upl"], ["sur"])
    op("v", lambda: V.tensor_copy(T.twt[:, :], T.twi[:, :]), ["twi"], ["twt"])

    def limits():
        for a in (1, 2):
            c = 32 * (a - 1)
            op("v", lambda: V.tensor_scalar(T.msh[:, c:c + 32], T.ibm[:, 64:96], 4 - a, None, Op.arith_shift_right), ["ibm"], ["msh%d" % a])
        for a in (1, 2):
            c, m = 32 * (a - 1), 16 * (a - 1)
            op("v", lambda: V.tensor_tensor(T.mdf[:, m:m + 16], T.msh[:, c:c + 16], T.msh[:, c + 16:c + 32], Op.subtract), ["msh%d" % a], ["mdf%d" % a])
        op("v", lambda: V.tensor_scalar(T.mdg[:, :], T.mdf[:, :], HUGE, None, Op.mult), ["mdf1", "mdf2"], ["mdg"])
        for a in (1, 2):
            m = 16 * (a - 1)
            op("v", lambda: V.tensor_tensor(T.m16[:, 16 * a:16 * a + 16], T.mdg[:, m:m + 16], T.m16[:, 0:16], Op.add), ["mdg", "m160"], ["m16%d" % a])

    def zeros(a):
        m = 2 * COUNT[a]
        op("g", lambda: g.iota(T["et%d" % a][:, m:512], [[0, 512 - m]], 0, 0, allow_small_or_imprecise_dtypes=True), [], ["et%dz" % a])

    def slots(t):
        L, h, cn = LANES[t], LANES[t] // 2, T["cn%d" % t]
        A = 16 + 16 // L
        k = "cn%d" % t
        op("g", lambda: g.iota(cn[:, :], [[h, A], [1, L]], PLACES + h * (1 - 16 // L), 0, allow_small_or_imprecise_dtypes=True), [], [k])
        op("g", lambda: g.affine_select(cn[:, :], cn[:, :], [[0, A], [-1, L]], Op.is_ge, 0.0, h - 1, 0), [k], [k])
        op("g", lambda: g.iota(cn[:, L * (A - 1):L * (A - 1) + h], [[1, h]], PLACES, 0, allow_small_or_imprecise_dtypes=True), [k], [k])

    for t in range(ROUNDS):
        L, h, N = LANES[t], LANES[t] // 2, COUNT[t]
        C, M = N // 16, N // 2
        qx, sx, xt = T["qx%d" % t], T["sx%d" % t], T["xt%d" % t]
        kq, ksx = "qx%d" % t, "sx%d" % t
        ct, lct, mx, bt = T["ct%d" % t], T["lct%d" % t], T["mx%d" % t], T["bt%d" % t]
        kct, kbt = ["ct%d%s" % (t, a) for a in ("a", "b", "c")], "bt%d" % t
        xk = ["xt0"] if t == 0 else ["xt%d.%s" % (t, b) for b in ("f0", "f3", 1, 2, 3)]
        op("v", lambda: V.quantize_mx(qx[:, 0:256], sx[:, 0:256], xt[:, 0:1024]), xk, [kq, ksx])
        if t == 0:
            op("v", lambda: V.quantize_mx(T.qc[:, 0:512], T.scc[:, 0:512], T.cz[:, 0:2048]), ["cz0", "cz1", "cz2", "cz3"], ["qc", "scc"])
        else:
            op("v", lambda: V.tensor_tensor(bt[:, :], T.bta[:, 0:N], T.btb[:, 0:N], Op.add), ["bta", "btb"], [kbt])
        if t == 1:
            op("v", lambda: V.quantize_mx(T.qv[:, 0:128], T.sv[:, 0:128], T.vt[:, 0:512]), ["vt"], ["qv", "sv"])
        for a in range(2):
            op("p", lambda: P.matmul_mx(T.pg[:, 512 * a:512 * a + 128], T.qur[:, 0:128], T.sur[:, 0:128],
                                        qx[:, 128 * a:128 * a + 128], sx[:, 128 * a:128 * a + 128], True, True),
               ["qur", "sur", kq, ksx], ["pg%d" % a])

        def scales():
            send(T["lsx%d" % t][:, 0:256], sx[:, 0:256], "ax%d" % t, [ksx], scales_by)
        if t == 0:
            scales()
        send(T["lqx%d" % t][:, 0:256].bitcast(dt.uint8), qx[:, 0:256].bitcast(dt.uint8), "ax%d" % t, [kq], codes_by)
        if t:
            scales()
        else:
            slots(0)
        op("s", lambda: S.activation(T.sco[:, 0:128], T.pg[:, 0:128], COPY), ["pg0"], ["sco0"])
        op("v", lambda: V.tensor_copy(T.sco[:, 128:256], T.pg[:, 512:640]), ["pg1"], ["sco1"])
        if t == 0:
            lt, kl, w, w0, lo, st, dg, kd = T.twt, ["twt"], 256, 128, 0, 1, T.dg1, "dg1"
        else:
            lt, kl, w, lo, st, dg, kd = T["ct%d" % (t - 1)], ["ct%d%s" % (t - 1, a) for a in ("a", "b", "c")], COUNT[t - 1] + 16, 16, 2, T.dg2, "dg2"
            w0 = 16 * (C + 2 - C % 2)
        for a, x, y in ((0, 0, w0), (1, w0, w)):
            op("v", lambda: V.tensor_tensor(T.km[:, x:y], T.sco[:, 0:256].indirect(lt[:, x // 16:y // 16]), dg[:, x:y], Op.mult),
               ["sco0", "sco1", kd] + kl, ["km%d" % a])
        op("s", lambda: S.activation(T.uu[:, 0:w], T.sco[:, 0:256].indirect(lt[:, 0:w // 16]), COPY), ["sco0", "sco1"] + kl, ["uu"])
        if t == 0:
            op("s", lambda: S.activation(T.mx0[:, :], T.m16[:, 0:16].indirect(T.kapu[:, 0:16]), COPY), ["m160", "kapu"], ["mx0"])
            op("s", lambda: S.activation(T.bt0[:, :], T.win2[:, 0:256].indirect(T.twt[:, 0:16]), COPY), ["ramp", "twt"], ["bt0"])
        hc, N2 = C // 2, N // 2
        halves = [(0, 0, hc, 0, N2), (1, hc, C, N2, N)]
        for a, c0, c1, n0, n1 in halves:
            op("v", lambda: V.tensor_tensor_scan(T.ks[:, n0:n1], T.rs[:, n0:n1], T.km[:, lo + st * n0:lo + st * n1:st], 0.0, Op.mult, Op.add),
               ["rs", "km0", "km%d" % a], ["ks%d" % a])
        for a, c0, c1, n0, n1 in halves:
            op("v", lambda: V.tensor_tensor(T.dd[:, n0:n1], T.ks[:, n0:n1].indirect(T.rept[:, 0:hc]), T.uu[:, lo + st * n0:lo + st * n1:st], Op.subtract),
               ["ks%d" % a, "rept", "uu"], ["dd%d" % a])
        for a, c0, c1, n0, n1 in halves:
            op("v", lambda: V.tensor_tensor(T.cmp[:, n0:n1], T.dd[:, n0:n1], mx[:, n0:n1], Op.is_lt), ["dd%d" % a, "mx%d" % t], ["cmp%d" % a])
        for a, c0, c1, n0, n1 in halves:
            op("v", lambda: V.tensor_tensor_scan(T.pos[:, n0:n1], T.rs[:, n0:n1], T.cmp[:, n0:n1], 0.0, Op.mult, Op.add), ["rs", "cmp%d" % a], ["pos%d" % a])
        for a, c0, c1, n0, n1 in halves:
            op("v", lambda: V.tensor_copy(T.post[:, c0:c1], T.pos[:, n0 + 15:n1:16]), ["pos%d" % a], ["post%d" % a])
        for a, c0, c1, n0, n1 in halves:
            op("v", lambda: V.tensor_tensor(T.sel[:, n0:n1], T.win[:, 16 * t:16 * t + 16].indirect(T.post[:, c0:c1]), bt[:, n0:n1], Op.mult),
               ["win", "post%d" % a, kbt], ["sel%d" % a])
        for a, c0, c1, n0, n1 in halves:
            op("v", lambda: V.tensor_tensor_scan(T.ses[:, n0:n1], T.rs[:, n0:n1], T.sel[:, n0:n1], 0.0, Op.mult, Op.add), ["rs", "sel%d" % a], ["ses%d" % a])
        op("v", lambda: V.tensor_copy(ct[:, 1:hc + 1], T.ses[:, 15:N2:16]), ["ses0"], [kct[0]])
        op("v", lambda: V.tensor_copy(ct[:, hc + 1:C + 1], T.ses[:, N2 + 15:N:16]), ["ses1"], [kct[1]])
        op("v", lambda: V.tensor_copy(ct[:, 0:1], T.ses[:, N - 1:N]), ["ses1"], [kct[2]])
        send(lct[:, :], ct[:, :], "al%d" % t, kct, topo.engines(core, nxt))
        if t == 0:
            slots(1)
            slots(2)
            zeros(1)
            zeros(2)

        for b in range(4):
            op("p", lambda: P.matmul_mx(T.pf[:, 512 * b:512 * b + 256], T.qc[:, 128 * b:128 * b + 128], T.scc[:, 128 * b:128 * b + 128],
                                        qx[:, 0:256], sx[:, 0:256], True, True), ["qc", "scc", kq, ksx], ["pf%d" % b])

        def window(b):
            op("s", lambda: S.activation(T.vw[:, 384 * b:384 * b + 256], T.pf[:, 512 * b:512 * b + 256], COPY), ["pf%d" % b], ["vwf%d" % b])
        for b in (0, 1, 2):
            window(b)
        if t == 0:
            op("s", lambda: S.activation(T.dg2[:, :], T.win[:, 48:64].indirect(T.dgl[:, 0:17]), COPY), ["win", "dgl"], ["dg2"])

        arrive("ax%d" % t, n_state, ["lqx%d" % t])

        def arrived(b, q):
            dst, src = T.fp[:, 256 * b:256 * b + 256], T.pg[:, 512 * b:512 * b + 256]
            op(q, lambda: V.tensor_copy(dst, src) if q == "v" else S.activation(dst, src, COPY), ["pg%d" % b], ["fp%d" % b])
        for b in range(4):
            op("p", lambda: P.matmul_mx(T.pg[:, 512 * b:512 * b + 256], T.qc[:, 128 * b:128 * b + 128], T.scc[:, 128 * b:128 * b + 128],
                                        T["lqx%d" % t][:, 0:256], T["lsx%d" % t][:, 0:256], True, True), ["qc", "scc", "lqx%d" % t], ["pg%d" % b])

        def renewed():
            op("s", lambda: S.activation(T.win2[:, 256:256 + N], T.vwx[:, 0:N + 16].indirect(T.et[:, 0:C]), COPY), ["vwx", "et"], ["val"])
        op("v", lambda: V.tensor_tensor(T.ef[:, 0:C], T.pos[:, 15:N:16], T.i16[:, 0:C], Op.add), ["pos0", "pos1", "i16"], ["ef"])
        if t < ROUNDS - 1:
            ctr, kr = T["ctr%d" % (t + 1)], "ctr%d" % (t + 1)
            op("s", lambda: S.activation(ctr[:, :], T.win2[:, 0:256].indirect(ct[:, 0:C + 1]), COPY), ["ramp"] + kct, [kr])
            op("s", lambda: S.activation(T.bta[:, 0:M], ctr[:, 16:16 + N:2], COPY, scale=T.loc[:, 0:1]), [kr, "loc"], ["bta"])
            op("s", lambda: S.activation(T.btb[:, 0:M], ctr[:, 17 - L:17 - L + N:2], COPY, scale=T.upc[:, 0:1]), [kr, "upc"], ["btb"])
        upt = T["upt%d" % (t + 1)]
        if t == 0:
            op("v", lambda: V.tensor_scalar(T.et[:, 0:C], T.ef[:, 0:C], float(16 - h), None, Op.add), ["ef"], ["et"])
            op("v", lambda: V.tensor_tensor(T.vwx[:, 0:N + 16], ctr[:, :].indirect(T.lnk[:, 0:C + 1]), T.cn0[:, :], Op.max), [kr, "lnk", "cn0"], ["vwx"])
            renewed()
            limits()
            for a in (1, 2):
                op("s", lambda: S.activation(T["mx%d" % a][:, :], T.m16[:, 16 * a:16 * a + 16].indirect(T.kapu[:, 0:COUNT[a] // 16]), COPY),
                   ["m16%d" % a, "kapu"], ["mx%d" % a])
            for b in (0, 1, 2):
                arrived(b, "s")
            op("v", lambda: V.tensor_copy(T.ur[:, 0:256].indirect(T.twt[:, 0:16]), T.win2[:, 256:512]), ["val", "twt"], ["ur"])
            op("v", lambda: V.tensor_tensor(T.um[:, :], T.ur[:, :], T.dg1[:, :], Op.mult), ["ur", "dg1"], ["um"])
            arrived(3, "v")
        else:
            for b in (0, 1, 2):
                arrived(b, "s")
            cb, brow = T["cb%d" % t], T["ctr%d" % t][:, 16:16 + 2 * N:2]
            op("v", lambda: V.tensor_tensor(T.sel2[:, 0:N], T.win[:, 48:64].indirect(T.post[:, 0:C]), brow, Op.mult), ["win", "post0", "post1", "ctr%d" % t], ["sel2"])
            op("v", lambda: V.tensor_scalar(T.et[:, 0:C], T.ef[:, 0:C], float(16 - h), None, Op.add), ["ef"], ["et"])
            op("v", lambda: V.tensor_tensor_scan(T.ses2[:, 0:N], T.rs[:, 0:N], T.sel2[:, 0:N], 0.0, Op.mult, Op.add), ["rs", "sel2"], ["ses2"])
            op("v", lambda: V.tensor_copy(cb[:, 1:C + 1], T.ses2[:, 15:N:16]), ["ses2"], ["cba"])
            op("v", lambda: V.tensor_copy(cb[:, 0:1], T.ses2[:, N - 1:N]), ["ses2"], ["cb"])
            op("v", lambda: V.tensor_tensor(T.vwx[:, 0:N + 16], T.win2[:, 0:256].indirect(cb[:, 0:C + 1]), T["cn%d" % t][:, :], Op.max),
               ["ramp", "cba", "cb", "cn%d" % t], ["vwx"])
            renewed()
            arrived(3, "v")
            op("v", lambda: V.tensor_tensor(T.um[:, :], T.win2[:, 0:256 + N].indirect(T["upt%d" % t][:, 0:16]), T.dg1[:, :], Op.mult),
               ["ramp", "val", "upt%d" % t, "dg1"], ["um"])

        arrive("al%d" % t, n_list, ["lct%d" % t])
        ee, ke = T["et%d" % t], "et%d" % t
        W = N + 16

        def ends(q, b):
            src = T.fp[:, 256 * b:256 * b + 256].indirect(lct[:, 0:C + 1])
            dst = T.fe[:, 272 * b:272 * b + W]
            op(q, lambda: V.tensor_copy(dst, src) if q == "v" else S.activation(dst, src, COPY), ["fp%d" % b, "lct%d" % t], ["fe%d" % b])

        def mean(b):
            op("v", lambda: V.tensor_tensor(ee[:, b:4 * M:4], T.fe[:, 272 * b + 16:272 * b + 16 + N:2],
                                            T.fe[:, 272 * b + 17 - L:272 * b + 17 - L + N:2], Op.add), ["fe%d" % b], [ke + ".%d" % b])
        ends("v", 3)
        for b in (0, 1, 2):
            ends("s", b)
        for b in (3, 0, 1, 2):
            mean(b)
        window(3)
        op("s", lambda: S.activation(T.f0[:, :], T.pf[:, 0:256], COPY), ["pf0"], ["f0"])
        op("s", lambda: S.activation(T.f3[:, :], T.pf[:, 1664:1792], COPY), ["pf3"], ["f3"])
        qe, se, kqe = T["qe%d" % t], T["se%d" % t], "qe%d" % t
        op("v", lambda: V.quantize_mx(qe[:, 0:128], se[:, 0:128], ee[:, 0:512]), [ke + ".%d" % b for b in range(4)] + ([ke + "z"] if t else []), [kqe])
        for b in (1, 0, 2, 3):
            op("p", lambda: P.matmul_mx(T.pg[:, 512 * b:512 * b + 128], T.wq[:, 128 * b:128 * b + 128], T.wsc[:, 128 * b:128 * b + 128],
                                        qe[:, 0:128], se[:, 0:128], True, True), ["wq", "wsc", kqe], ["pg%d" % b])
        op("v", lambda: V.tensor_tensor_scan(T.us[:, :], T.rs[:, :], T.um[:, :], 0.0, Op.mult, Op.add), ["rs", "um"], ["us"])
        op("v", lambda: V.tensor_copy(upt[:, :], T.us[:, 15:256:16]), ["us"], ["upt%d" % (t + 1)])
        xn = T["xt%d" % (t + 1)]
        kup = "upt%d" % (t + 1)

        def made(q, b):
            dst, src = T.vw[:, 384 * b + 256:384 * b + 256 + M], T.pg[:, 512 * b:512 * b + M]
            op(q, lambda: V.tensor_scalar(dst, src, 0.015625, None, Op.mult) if q == "v" else S.activation(dst, src, COPY, scale=0.015625),
               ["pg%d" % b], ["vwh%d" % b])
        made("s", 1)
        for b in (0, 2, 3):
            made("v", b)
        for b, n in ((1, 256), (2, 256), (3, 128)):
            op("s", lambda: S.activation(T.nr[:, 256 * b:256 * b + n], T.vw[:, 384 * b:384 * b + 256 + M].indirect(upt[:, 0:n // 16]), COPY),
               ["vwf%d" % b, "vwh%d" % b, kup], ["nr%d" % b])

        def both(b, x, f, k):
            op("v", lambda: V.tensor_tensor(xn[:, 4 * x + b:1024:4], T.vw[:, 384 * b:384 * b + 256 + M].indirect(upt[:, x // 16:16]), f[:, :], Op.add),
               ["vwf%d" % b, "vwh%d" % b, k, kup], ["xt%d.%s" % (t + 1, k)])

        def blend(b, n):
            op("v", lambda: V.tensor_tensor(xn[:, b:4 * n:4], T.pf[:, 512 * b:512 * b + n], T.nr[:, 256 * b:256 * b + n], Op.add),
               ["pf%d" % b, "nr%d" % b], ["xt%d.%d" % (t + 1, b)])
        both(0, 0, T.f0, "f0")
        blend(1, 256)
        both(3, 128, T.f3, "f3")
        blend(2, 256)
        blend(3, 128)
        if t == ROUNDS - 1:
            op("v", lambda: V.quantize_mx(T.qx3[:, 0:256], T.sx3[:, 0:256], xn[:, 0:1024]), ["xt3.%s" % b for b in ("f0", "f3", 1, 2, 3)], ["qx3", "sx3"])
            op("s", lambda: S.activation(T.urow[:, :], T.win2[:, 0:256 + N].indirect(T["upt%d" % t][:, 0:16]), COPY), ["ramp", "val", "upt%d" % t], ["urow"])
            op("y", lambda: Y.dma_start(T.op[:, :], T.urow[0:128:16, :]), ["urow"], [], "oo", 16)

    for a in range(2):
        op("p", lambda: P.matmul_mx(T.pg[:, 512 * a:512 * a + 128], T.qv[:, 0:128], T.sv[:, 0:128],
                                    T.qx3[:, 128 * a:128 * a + 128], T.sx3[:, 128 * a:128 * a + 128], True, True), ["qv", "sv", "qx3", "sx3"], ["pg%d" % a])
    op("y", lambda: Y.dma_start(T.oc[:, 0:1024], T.qx3[:, 0:256].bitcast(dt.uint8)), ["qx3"], [], "oa", 16)
    for k in range(4):
        op("y", lambda: Y.dma_start(T.osc[4 * k:4 * k + 4, 0:256], T.sx3[32 * k:32 * k + 4, 0:256]), ["sx3"], [], "oa", 16)
    op("v", lambda: V.tensor_copy(T.ysb[:, 0:128], T.pg[:, 0:128]), ["pg0"], ["ya"])
    op("s", lambda: S.activation(T.ysb[:, 128:256], T.pg[:, 512:640], COPY), ["pg1"], ["yb"])
    op("y", lambda: Y.dma_start(T.y[:, 0:128], T.ysb[:, 0:128]), ["ya"], [], "oa", 16)
    op("s", lambda: S.dma_start(T.y[:, 128:256], T.ysb[:, 128:256]), ["yb"], [], "ob", 16)

    for sem in count:
        if waited.get(sem, 0) < count[sem]:
            g.wait_ge(T.sem[sem], count[sem])
